import numpy as np, ml_dtypes
CORES = [10,34,74,98]
N = 4
import mx_ref
BF = ml_dtypes.bfloat16
def gentries(a):
    return np.ascontiguousarray(a.reshape(8, 16, -1).transpose(0, 2, 1)).reshape(8, -1)
def gtable(e):
    e = np.asarray(e); return np.ascontiguousarray(e.reshape(8, -1, 16).transpose(0, 2, 1)).reshape(128, -1).astype(np.int32)
def gcols(t, e):
    v = np.concatenate([t.reshape(8, 16, -1, 4), np.zeros((8, 16, 1, 4), BF)], axis=2)
    return np.ascontiguousarray(np.stack([v[g][:, e[g]] for g in range(8)])).reshape(128, -1)
def pick(q, e):
    c = np.concatenate([q[0].reshape(128, -1, 4), np.zeros((128, 1, 4), np.uint8)], axis=1); s = np.concatenate([q[1], np.ones((16, 1), np.uint8)], axis=1)
    return (np.ascontiguousarray(c[:, e].reshape(128, -1)), np.ascontiguousarray(s[:, e]))
def join(*qs):
    return (np.concatenate([q[0] for q in qs], axis=1), np.concatenate([q[1] for q in qs], axis=1))
def put(q, e, v):
    c, s = q[0].reshape(128, -1, 4).copy(), q[1].copy(); c[:, e] = v[0].reshape(128, -1, 4); s[:, e] = v[1]
    return (c.reshape(128, -1), s)
def pk(c, s):
    return (np.ascontiguousarray(c), mx_ref.live(s))
def emit(q):
    return q[0], q[1]
def packed(v, rng):
    q = [mx_ref.quantize(np.ascontiguousarray(v[r])) for r in range(N)]
    return np.stack([a for a, b in q]), np.stack([mx_ref.plane(b, rng) for a, b in q])
def values_of_codes():
    e, c = np.zeros((128, 128, 4), np.float32), np.zeros((128, 2, 4), np.uint8)
    e[np.arange(128), np.arange(128), 0] = 1
    c[:127, :, 0] = np.arange(256).reshape(2, 128).T[:127]
    return mx_ref.matmul(mx_ref.quantize(e.reshape(128, 512).astype(BF)), (c.reshape(128, 8), np.full((16, 2), 127, np.uint8))).T.reshape(-1).astype(np.float64)
CODE_VALUE, SCALE_VALUE = values_of_codes(), 2.0 ** (np.arange(256) - 127.0)
def decode(q):
    return (CODE_VALUE[q[0]].reshape(16, 8, -1, 4) * SCALE_VALUE[q[1]][:, None, :, None] + 0.0).reshape(128, -1).astype(np.float32)
def f(rng, *shape):
    return mx_ref.flush((rng.standard_normal(shape, dtype=np.float32) * np.exp2(rng.integers(-2, 3, shape[:-1] + (1,)))).astype(BF))
def wide(rng, *shape, cols=0):
    v = rng.standard_normal(shape, dtype=np.float32) * np.exp2(rng.integers(-12, 13, shape)).astype(np.float32)
    if cols: v *= np.repeat(np.exp2(rng.integers(-cols, cols + 1, shape[:-2] + (1, shape[-1] // 4))) * (rng.random(shape[:-2] + (1, shape[-1] // 4)) > 0.0625), 4, axis=-1).astype(np.float32)
    return mx_ref.flush(v.astype(BF))
C, M, R = 384, 160, 3
def numbers_of(rng):
    return {"x": np.array(f(rng, N, 128, 4 * C)), "u": np.array(f(rng, N, 128, 512)), "v": np.array(f(rng, N, 128, 512))}
def shuffled(rng):
    return np.argsort(rng.random((N, 8, C)), axis=2)
def stored(t):
    return {"cf": np.stack([gtable(t[r]) for r in range(N)])}
def weights(rng, w):
    c, p = packed(np.ascontiguousarray(w).reshape(N, 128, 2048), rng)
    return {"wc": c, "ws": p}
def layers(rng, still=[]):
    w = np.array(f(rng, N, 128, 2048)).reshape(N, 8, 16, 4, 8, 16, 4)
    for i in still:
        w[:, :, i] = 0
        w[:, :, :, :, :, i] = 0
    return weights(rng, w)
def setup_inputs(rng):
    return {**numbers_of(rng), **stored(shuffled(rng)), **layers(rng)}
def setup_inputs_ties(rng):
    d = numbers_of(rng)
    x = d["x"].reshape(N, 8, 16, C, 4)
    x[:, :, :2] = 0
    x[:, :, 0, :, 0] = rng.integers(0, 4, (N, 8, C)).astype(np.float32).astype(BF)
    x[:, :, 1, :, 0] = rng.integers(0, 3, (N, 8, C)).astype(np.float32).astype(BF)
    u = d["u"].reshape(N, 128, 128, 4)
    u[:, :, ::16] = 0
    u[:, :, 1] = 0
    o = rng.permutation(N)
    for r in range(N):
        s = 0.0 if r == o[0] else -1.0 if r == o[1] else 1.0
        for h in range(0, 128, 16): u[r, h, h, 0] = s
        u[r, 1, 1, 0] = s
    return {"x": x.reshape(N, 128, 4 * C), "u": u.reshape(N, 128, 512), "v": d["v"], **stored(shuffled(rng)), **layers(rng, [0, 1])}
def setup_inputs_near(rng):
    d = numbers_of(rng)
    o = rng.permutation(N) % 4
    c = np.where(o % 2 == 0, 1.0, -1.0)
    x = d["x"].astype(np.float32).reshape(N, 8, 16, C, 4)
    x[:, :, 0] = 0
    x[:, :, 8:] = 0
    x[:, :, 0, :, 0] = c[:, None, None]
    s = rng.integers(0, 16, (N, 8, C))
    x[:, :, 8] = ((s[:, :, :, None] >> np.arange(4)) & 1) * np.exp2(np.arange(4) - 23.0)
    x[:, :, 11, :, 0] = 2.0 ** -10
    u = d["u"].reshape(N, 128, 128, 4)
    u[:, :, ::16] = 0
    u[:, :, 1] = 0
    for r in range(N):
        for g in 1 + rng.permutation(7)[:4]: x[r, g, 0, rng.integers(C), 0] = c[r] * 2.0 ** 29
        if o[r] == 1: x[r, 0, 0, rng.integers(C), 0] = -2.0 ** 29
        if o[r] == 3:
            i = rng.integers(0, 2, (8, C))
            x[r, :, 8:] = 0
            x[r, :, 10, :, 0] = (1.0 + 0.125 * i) * 2.0 ** -30
            x[r, :, 12, :, 0] = (1.125 - 0.125 * i) * 2.0 ** -30
        k = 2.0 ** -30 if o[r] == 2 else 1.0
        for a, h in [(0, 1)] + [(h, h) for h in range(0, 128, 16)]:
            if o[r] == 3:
                u[r, a + 10, h, 0] = 1.125 * 2.0 ** -30
                u[r, a + 12, h, 0] = 2.0 ** -30
            else:
                u[r, a, h, 0] = k
                u[r, a + 8, h] = k
                u[r, a + 11, h, 0] = k
    return {"x": x.reshape(N, 128, 4 * C).astype(BF), "u": u.reshape(N, 128, 512), "v": d["v"], **stored(shuffled(rng)), **layers(rng, [0] + [8, 9, 10, 11, 12, 13, 14, 15])}
def swings(rng):
    h, j, a = np.zeros(C, int), 0, 200
    while j < C:
        i = np.arange(min(int(rng.integers(10, 25)), C - j))
        n = np.where((i > 8) & (rng.random(len(i)) < 0.25), rng.integers(2, np.maximum(i, 3)), i)
        h[j:j + len(i)] = (1 - 2 * (i % 2)) * (a - 8 * n)
        j, a = j + len(i), a + 1
    return h
def setup_inputs_deep(rng):
    d = numbers_of(rng)
    x = d["x"].reshape(N, 8, 16, C, 4)
    o = rng.permutation(N)
    t = np.arange(C) - C // 2
    small = (1.0 + (2 * rng.integers(0, 64, (N, 8, 8, C, 4)) + 1) * 2.0 ** -7) * np.exp2(-rng.integers(8, 15, (N, 8, 8, C, 4)).astype(np.float64))
    small = small * rng.choice([-1.0, 1.0], small.shape)
    small[:, :, 0, :, 0] = np.where(rng.random((N, 8, C)) < 0.5, 1.875, 1.96875)
    x[:, :, 8:] = small.astype(np.float32).astype(BF)
    x[:, 0, 0] = 0
    u = d["u"].reshape(N, 128, 128, 4)
    u[:, :, 1] = 0
    u[:, 0, 1, 0] = 16
    u[:, 0, 1, 1] = 1
    for r in range(N):
        h = t if r == o[0] else -t if r == o[1] else swings(rng)
        x[r, 0, 0, :, 0] = (np.sign(h) * (np.abs(h) // 16)).astype(np.float32).astype(BF)
        x[r, 0, 0, :, 1] = (np.sign(h) * (np.abs(h) % 16)).astype(np.float32).astype(BF)
    return {"x": x.reshape(N, 128, 4 * C), "u": u.reshape(N, 128, 512), "v": d["v"], **stored(shuffled(rng)), **layers(rng)}
def setup_inputs_ends(rng):
    d = numbers_of(rng)
    o = (np.arange(N) + int(rng.integers(N))) % 4
    x = np.zeros((N, 8, 16, C, 4))
    u = d["u"].reshape(N, 128, 128, 4)
    u[:, :, ::16] = 0
    t = shuffled(rng)
    w = np.zeros((N, 128, 4, 128, 4), np.float32)
    i = np.arange(128)
    for r in range(N):
        sign = rng.permutation(8) % 2 * 2.0 - 1.0
        wave = 2.0 ** 30 * (0.9 + 0.1 * rng.random((128, 8, 4)))
        u[r, :, 1] = 2.0 ** -30 if o[r] == 3 else 2.0 ** 30
        if o[r] == 0:
            x[r] = -2.0 ** 30 * (0.9 + 0.1 * rng.random((8, 16, C, 4)))
            u[r, :, ::16] = wave.astype(np.float32).astype(BF)
            t[r] = np.arange(C)
        if o[r] == 1:
            x[r] = 2.0 ** 30 * np.where(rng.random((8, 16, C, 4)) < 0.125, 0.8125, 0.875) * (rng.permutation(C) % 2 * 2.0 - 1.0)[:, None]
            u[r, :, ::16] = (wave * sign[:, None]).astype(np.float32).astype(BF)
            for b in range(4): w[r, i, b, i, b] = rng.choice([-1.0, 1.0], 128)
        if o[r] == 2:
            x[r] = 2.0 ** 30
            x[r, rng.permutation(8)[:4]] *= np.where(rng.random((4, 1, C, 1)) < 0.5, 0.875, 1.0)
            t[r] = np.arange(C)[::-1]
            for g in range(8): u[r, 16 * g:16 * g + 16, 16 * g] = sign[g] * 2.0 ** 30
        if o[r] == 3:
            x[r] = 2.0 ** -30 * (1.0 + 0.125 * rng.integers(0, 8, (8, 16, C, 4)))
            t[r, ::2] = np.arange(C)
            t[r, 1::2] = np.arange(C)[::-1]
            for g in range(8): u[r, 16 * g:16 * g + 16, 16 * g] = 2.0 ** -30
    d["v"] = (np.where(d["v"] < 0, -1.0, 1.0) * np.where(rng.permutation(N) % 2, 2.0 ** -30, 2.0 ** 30)[:, None, None]).astype(np.float32).astype(BF)
    return {"x": x.astype(np.float32).reshape(N, 128, 4 * C).astype(BF), "u": u.reshape(N, 128, 512), "v": d["v"], **stored(t), **weights(rng, w.astype(BF))}
def setup_inputs_spread(rng):
    d = setup_inputs(rng)
    d["x"] = wide(rng, N, 128, 4 * C, cols=6)
    return d
def check_inputs(d):
    b = []
    for k in ("x", "u", "v"):
        a = np.abs(d[k].astype(np.float32))
        if not (np.isfinite(a).all() and ((a == 0) | (a >= 2.0 ** -30) & (a <= 2.0 ** 30)).all()): b.append("a value of " + k)
    none, least, most = [emit(mx_ref.quantize(np.full((128, 16), k, np.float32).astype(BF)))[1][0, 0] for k in (0.0, 2.0 ** -30, 2.0 ** 30)]
    for r in range(N):
        if (np.sort(gentries(d["cf"][r]), axis=1) != np.arange(C)).any(): b.append("cf: a group hasn't every column once")
        if ((d["wc"][r] == 0x7F) | (d["wc"][r] == 0xFF)).any(): b.append("wc: a code that is no number")
        s = mx_ref.live(d["ws"][r])
        if ((s != none) & ((s < least) | (s > most))).any(): b.append("ws: a scale out of range")
    return b
def turning(h):
    t = np.arange(C)
    e, found = np.zeros(C, np.int64), []
    for i in range(7):
        inside = (t >= e[:, None]) & (t <= t[:, None])
        s = np.where(inside, h if i % 2 == 0 else -h, np.float32(-np.inf))
        e = C - 1 - np.argmax(s[:, ::-1], axis=1)
        found.append(e)
    found = np.stack(found + [t])
    return found, np.argmax(found == t, axis=0)
def reference(x, u, v, cf, wc, ws):
    qu = [mx_ref.quantize(u[r]) for r in range(N)]
    lay = [pk(wc[r], ws[r]) for r in range(N)]
    now = [x[r] for r in range(N)]
    reads = [gentries(cf[r]) for r in range(N)]
    for t in range(R):
        blend, low, sent = [], [], []
        for r in range(N):
            q = mx_ref.quantize(now[r])
            own = decode(q).astype(BF)
            s = mx_ref.matmul(qu[r], q) + np.float32(0.0)
            e, depth = turning(s[1])
            at = np.take_along_axis(e, np.maximum(depth - np.arange(9)[:, None], 0), axis=0)
            a = np.take_along_axis(reads[r], at[:8], axis=1)
            b = np.take_along_axis(reads[r], at[1:], axis=1)
            z = ((gcols(own, a).astype(np.float32) + gcols(own, b).astype(np.float32)) * np.float32(0.5)).astype(BF)
            o = np.argsort(-s[::16], axis=1, kind="stable")
            l, d = o[:, :M], o[:, C - M:]
            sent.append(mx_ref.quantize(gcols(z, l)))
            other = np.tile(np.arange(C), (8, 1))
            np.put_along_axis(other, l, d, axis=1)
            np.put_along_axis(other, d, l, axis=1)
            reads[r] = np.take_along_axis(other, reads[r], axis=1)
            blend.append(z)
            low.append(d)
        for r in range(N):
            came = sent[(r - 1) % N]
            made = np.stack([mx_ref.matmul(pick(lay[r], np.arange(128 * b, 128 * b + 128)), came) * np.float32(0.03125) for b in range(4)], axis=2).reshape(8, 16, M, 4)
            z = blend[r].astype(np.float32).reshape(8, 16, C, 4)
            for g in range(8): z[g][:, low[r][g]] = made[g] + z[g][:, low[r][g]]
            now[r] = z.reshape(128, 4 * C).astype(BF)
    y, op = np.zeros((N, 128, C), np.float32), np.zeros((N, 8, C), np.float32)
    oc, osc = np.zeros((N, 128, 4 * C), np.uint8), np.zeros((N, 16, C), np.uint8)
    for r in range(N):
        q = mx_ref.quantize(now[r])
        y[r] = mx_ref.matmul(mx_ref.quantize(v[r]), q)
        op[r] = reads[r]
        oc[r], osc[r] = emit(q)
    return {"y": y, "op": op, "oc": oc, "osc": osc}

@@ -1,0 +1,445 @@
+from concourse.mybir import dt, AluOpType, ActivationFunctionType
+
+C, M, ROUNDS = 384, 160, 3
+FIRST = 4
+WIDE = [max(128, 64 * (i + 1)) for i in range(6)]
+X4 = "float8_e4m3fn_x4"
+F32, BF = "float32", "bfloat16"
+SCRATCH = {}
+
+
+def _buf(name, cols, dtype, where="sbuf"):
+    SCRATCH[name] = (where, [128, cols], dtype)
+
+
+def _pair(name, cols):
+    _buf(name + "_q", cols, X4)
+    _buf(name + "_s", cols, "uint8")
+
+
+for _n, _c in (("xb", 4 * C), ("ub", 512), ("vb", 512), ("cb", 8 * 512), ("sig", 8 * C), ("sgn", 3 * C), ("le", 4 * C),
+               ("ge", 4 * C), ("mk", 8 * C), ("junk", 4 * C), ("eb", 4 * M), ("ones", C), ("km", C), ("kf", C), ("foldb", C)):
+    _buf(_n, _c, BF)
+for _n, _c in (("fp", BF), ("fc", BF), ("ag", BF), ("zp", BF), ("rz", F32)):
+    _buf(_n, 4 * C, _c)
+for _i in range(6):
+    _buf("cmp%d" % _i, 4 * WIDE[_i], BF)
+for _n, _c in (("iotaj", C), ("crow", C), ("jmod", 2 * C), ("g8", 512), ("e4", 512), ("jt", 48), ("jg", 48), ("ct0", 24),
+               ("qg", 8), ("mask", 2 * C), ("fold0", 2 * C), ("mbig", C), ("hs", 4), ("ka", C), ("win", 8 * C), ("u1", 48),
+               ("u2", 48), ("ab", 2 * C), ("abf", 2 * C), ("sm", C), ("sf", C), ("smk", C), ("rs", 24), ("ns", 24),
+               ("half", 4), ("rc", 24), ("cm", C), ("cf2", C), ("posf", 24), ("inv", C), ("lm", M), ("lf", M), ("wrow", C),
+               ("swap", C), ("crm", C), ("crf", C), ("yb", C)):
+    _buf(_n, _c, F32)
+for _n, _c in (("cfi", 24), ("pcol", 4), ("us32", 8), ("ti", 48), ("ti2", 48)):
+    _buf(_n, _c, "int32")
+for _n, _c in (("uso", 8), ("uho", 8), ("oab", 48), ("at", 48), ("pos", 24), ("lo", 10), ("cl", 24)):
+    _buf(_n, _c, "uint16")
+for _n, _c in (("u", 128), ("us", 128), ("uh", 128), ("v", 128), ("w", 512), ("x", C), ("k", 8 * 128), ("le", C), ("ge", C),
+               ("mk", 2 * C)):
+    _pair(_n, _c)
+for _i in range(6):
+    _pair("cmp%d" % _i, WIDE[_i])
+for _r in range(ROUNDS):
+    _pair("e%d" % _r, M)
+    _pair("land%d" % _r, M)
+for _b in range(8):
+    _buf("ps%d" % _b, 512, F32, "psum")
+SEMAPHORES = ["vec", "act", "ten", "pool", "sent", "ldx", "ldu", "ldv", "ldw", "lds", "ldc", "sty", "stp", "stc",
+              "sts0", "sts1", "sts2", "sts3", "arr0", "arr1", "arr2"]
+
+LT, LE, GE, EQ = AluOpType.is_lt, AluOpType.is_le, AluOpType.is_ge, AluOpType.is_equal
+ADD, SUB, MUL, MAX, MIN = AluOpType.add, AluOpType.subtract, AluOpType.mult, AluOpType.max, AluOpType.min
+COPY, SIGN = ActivationFunctionType.Copy, ActivationFunctionType.Sign
+ABS, RELU = ActivationFunctionType.Abs, ActivationFunctionType.Relu
+EB0, SG, K512, K3, SGH = 0, 4, 5, 6, 7
+
+
+def rank_program(g, core, T, topo):
+    rank = T.rank_of(core)
+    if rank is None:
+        return
+    queue = {"v": g.vector, "s": g.scalar, "t": g.tensor, "p": g, "y": g.sync}
+    own = {"v": "vec", "s": "act", "t": "ten", "p": "pool"}
+    count = {"vec": 0, "act": 0, "ten": 0, "pool": 0}
+    seen = {q: {} for q in queue}
+    clock, hist = {}, {}
+
+    def waits(q, reads, writes):
+        need = {}
+        for kind, regs in (("r", reads), ("w", writes)):
+            for key, lo, hi in regs:
+                for a, b, k, q2, ev in hist.get(key, []):
+                    if b <= lo or hi <= a:
+                        continue
+                    if kind == "r" and k == "r" and not (key[:2] == "ps" and q2 != q):
+                        continue
+                    if kind == "w" and q2 == q and (k == "r" or q == "t"):
+                        continue
+                    need[ev[0]] = max(need.get(ev[0], 0), ev[1])
+        need = {s: n for s, n in need.items() if seen[q].get(s, 0) < n}
+        for s in sorted(need):
+            if any(o != s and clock[(o, need[o])].get(s, 0) >= need[s] for o in need if need[o]):
+                need[s] = 0
+        for s, n in need.items():
+            if n and seen[q].get(s, 0) < n:
+                queue[q].wait_ge(T.sem[s], n)
+                for s2, n2 in clock[(s, n)].items():
+                    seen[q][s2] = max(seen[q].get(s2, 0), n2)
+
+    def note(q, ev, reads, writes):
+        clock[ev] = dict(seen[q] if q in seen else {})
+        clock[ev][ev[0]] = ev[1]
+        for key, lo, hi in writes:
+            hist[key] = [e for e in hist.get(key, []) if not (lo <= e[0] and e[1] <= hi)] + [(lo, hi, "w", q, ev)]
+        for key, lo, hi in reads:
+            hist[key] = [e for e in hist.get(key, []) if not (e[2] == "r" and e[3] == q and lo <= e[0] and e[1] <= hi)]
+            hist[key].append((lo, hi, "r", q, ev))
+
+    def full(regs):
+        return [(r, 0, 1 << 20) if not isinstance(r, tuple) else r for r in regs]
+
+    def run(q, reads, writes, call):
+        reads, writes = full(reads), full(writes)
+        waits(q, reads, writes)
+        s = own[q]
+        count[s] += 1
+        call().then_inc(T.sem[s], 1)
+        note(q, (s, count[s]), reads, writes)
+
+    def dma(q, sem, reads, writes, out, in_):
+        reads, writes = full(reads), full(writes)
+        waits(q, reads, writes)
+        queue[q].dma_start(out, in_).then_inc(T.sem[sem], 16)
+        saved = dict(seen[q])
+        note("d" + sem, (sem, 16), reads, writes)
+        clock[(sem, 16)].update(saved)
+
+    V, S, P = g.vector, g.scalar, g
+
+    def pl(buf, t):
+        return buf[:, C * t:C * t + C]
+
+    def codes(name, a, b):
+        return T[name + "_q"][:, a:b]
+
+    def plane(name, a, b):
+        return T[name + "_s"][:, a:b]
+
+    def quant(name, src, a=0, b=None, regs=None):
+        b = SCRATCH[name + "_q"][1][1] if b is None else b
+        run("v", [src] if regs is None else regs, [name + "_q"] if regs is None else [(name + "_q", a, b)],
+            lambda: V.quantize_mx(codes(name, a, b), plane(name, a, b), T[src][:, 4 * a:4 * b]))
+
+    def mm(bank, l, la, r, ra, rb, start=True, stop=True):
+        run("t", [(l + "_q", la, la + 128), (r + "_q", ra, rb)], ["ps%d" % bank],
+            lambda: g.tensor.matmul_mx(T["ps%d" % bank][:, 0:rb - ra], codes(l, la, la + 128), plane(l, la, la + 128),
+                                       codes(r, ra, rb), plane(r, ra, rb), start, stop))
+
+    def vts(reads, writes, out, in0, s1, s2, *ops):
+        run("v", reads, writes, lambda: V.tensor_scalar(out, in0, s1, s2, *ops))
+
+    def vtt(reads, writes, out, in0, in1, op):
+        run("v", reads, writes, lambda: V.tensor_tensor(out, in0, in1, op))
+
+    def vcp(reads, writes, out, in_):
+        run("v", reads, writes, lambda: V.tensor_copy(out, in_))
+
+    def act(reads, writes, out, in_, func=COPY, **kw):
+        run("s", reads, writes, lambda: S.activation(out, in_, func, **kw))
+
+    def scan(reads, writes, out, d0, d1, op0, op1):
+        run("v", reads, writes, lambda: V.tensor_tensor_scan(out, d0, d1, 0.0, op0, op1))
+
+    def fold(src, dst, n):
+        scan([src, "fold0"], [dst], T[dst][:, 0:n], T.fold0[:, 0:n], T[src][:, 0:n], MUL, ADD)
+
+    dma("y", "ldx", [], ["xb"], T.xb[:], T.x[:])
+    dma("s", "ldu", [], ["ub"], T.ub[:], T.u[:])
+    dma("s", "ldc", [], ["cfi"], T.cfi[:], T.cf[:])
+    dma("s", "ldw", [], ["w_q"], T.w_q[:, 0:512].bitcast(dt.uint8), T.wc[:])
+    dma("y", "lds", [], ["w_s"], T.w_s[:], T.ws[:])
+    dma("y", "ldv", [], ["vb"], T.vb[:], T.v[:])
+
+    def iota(name, a, b, pattern, base, cm, **kw):
+        run("p", [], [(name, a, b)], lambda: P.iota(T[name][:, a:b], pattern, base, cm, **kw))
+
+    def fill(name, a, b, value):
+        run("v", [], [(name, a, b)], lambda: V.memset(T[name][:, a:b], value))
+
+    def tile(k):
+        return "cb", 512 * k, 512 * k + 512
+
+    def const(k):
+        return T.cb[:, 512 * k:512 * k + 512]
+
+    ok = {"allow_small_or_imprecise_dtypes": True}
+    iota("us32", 0, 8, [[16, 8]], 0, 0)
+    iota("pcol", 0, 1, [[1, 1]], 0, 1)
+    iota("jmod", 0, 2 * C, [[0, 48], [1, 16]], 0, 0, **ok)
+    iota("g8", 0, 512, [[1, 8], [0, 64]], 0, 0, **ok)
+    iota("e4", 0, 512, [[1, 512]], 0, -4, **ok)
+    iota("crow", 0, C, [[1, C]], -512, 0, **ok)
+    iota("jt", 0, 24, [[16, 24]], 0, 0, **ok)
+    iota("jt", 24, 48, [[16, 24]], 0, 0, **ok)
+    for i in (5, 4, 3, 2, 1, 0):
+        iota("cmp%d" % i, 256 * i, 4 * WIDE[i], [[0, 4 * WIDE[i] - 256 * i]], 0, 0, **ok)
+    iota("iotaj", 0, C, [[1, C]], 0, 0, **ok)
+
+    fill("uho", 0, 8, 1)
+    fill(*tile(K512), 512.0)
+    fill(*tile(K3), 3.0)
+    vcp(["us32"], ["uso"], T.uso[:], T.us32[:])
+    vts(["pcol"], [("pcol", 1, 2)], T.pcol[:, 1:2], T.pcol[:, 0:1], 15, None, AluOpType.bitwise_and)
+    vts(["pcol"], [("pcol", 2, 3)], T.pcol[:, 2:3], T.pcol[:, 0:1], 4, None, AluOpType.arith_shift_right)
+    fill("ones", 0, C, 1.0)
+    vcp([("pcol", 1, 3)], [("qg", 0, 2)], T.qg[:, 0:2], T.pcol[:, 1:3])
+    fill("half", 0, 4, 0.5)
+    vts([("qg", 0, 2)], [("qg", 4, 6)], T.qg[:, 4:6], T.qg[:, 0:2], -1.0, None, MUL)
+    q_of, g_of = T.qg[:, 0:1], T.qg[:, 1:2]
+    act(["jmod"], ["fold0"], T.fold0[:], T.jmod[:], SIGN)
+    act(["jmod"], ["foldb"], T.foldb[:], T.jmod[:, 0:C], SIGN)
+    act(["jmod", ("qg", 4, 6)], ["mask"], T.mask[:], T.jmod[:], ABS, bias=T.qg[:, 4:5])
+    act(["mask"], ["mask"], T.mask[:], T.mask[:], RELU, bias=1.0, scale=-1.0)
+    act(["g8", ("qg", 4, 6)], ["g8"], T.g8[:], T.g8[:], ABS, bias=T.qg[:, 5:6])
+    act(["g8"], [tile(SG)], const(SG), T.g8[:], RELU, bias=1.0, scale=-1.0)
+    act(["g8"], [tile(SGH)], const(SGH), T.g8[:], RELU, bias=0.5, scale=-0.5)
+    quant("u", "ub")
+    for name, off in (("us", "uso"), ("uh", "uho")):
+        run("v", ["u_q", off], [name + "_q"],
+            lambda: V.tensor_copy(T[name + "_q"][:, 0:128].bitcast(dt.uint32), T.u_q[:, 0:128].bitcast(dt.uint32).indirect(T[off][:, 0:8])))
+        run("v", ["u_q", off], [name + "_q"],
+            lambda: V.tensor_copy(T[name + "_s"][:, 0:128], T.u_s[:, 0:128].indirect(T[off][:, 0:8])))
+    quant("x", "xb")
+    vts(["jmod", ("qg", 0, 2)], ["mbig"], T.mbig[:], T.jmod[:, 0:C], q_of, 2e29, LT, MUL)
+    for t in range(4):
+        vts(["e4"], [tile(EB0 + t)], const(EB0 + t), T.e4[:], float(t), 0.5, EQ, MUL)
+    vts(["mbig"], ["mbig"], T.mbig[:], T.mbig[:], 1e29, None, SUB)
+    quant("k", "cb", 0, 512, [("cb", 0, 2048)])
+    quant("k", "cb", 512, 1024, [("cb", 2048, 4096)])
+    for name, first in (("le", 3), ("ge", 3), ("mk", 4 * C + 3)):
+        run("v", [], [name], lambda: V.memset(T[name][:, first:first + 4 * C - 3:4], 0.0))
+    vcp(["cfi"], ["cl"], T.cl[:], T.cfi[:])
+
+    def tables():
+        lead = 4 * FIRST
+        vts(["jt", ("qg", 0, 2)], ["jt"], T.jt[:], T.jt[:], q_of, None, ADD)
+        vts([("qg", 0, 2)], [("qg", 2, 3)], T.qg[:, 2:3], g_of, 384.0, None, MUL)
+        vts([("qg", 0, 2)], [("qg", 3, 4)], T.qg[:, 3:4], g_of, 384.0, 384.0, MUL, ADD)
+        vts(["jt", ("qg", 2, 3)], [("jg", 0, 24)], T.jg[:, 0:24], T.jt[:, 0:24], T.qg[:, 2:3], None, SUB)
+        vts(["jt", ("qg", 3, 4)], [("jg", 24, 48)], T.jg[:, 24:48], T.jt[:, 24:48], T.qg[:, 3:4], None, SUB)
+        vts(["jt"], [("ct0", 0, lead)], T.ct0[:, 0:lead], T.jt[:, 0:lead], -1.0, 383.0 - 8 * (24 - lead), MUL, ADD)
+        vts(["jt", ("qg", 0, 2)], [("ct0", lead, 24)], T.ct0[:, lead:24], T.jt[:, lead:24], 0.0, q_of, MUL, SUB)
+        vts([("ct0", lead, 24)], [("ct0", lead, 24)], T.ct0[:, lead:24], T.ct0[:, lead:24], 199.0, None, ADD)
+        for t in range(4):
+            run("v", [], [("rz%d" % t, 0, C - M)], lambda: V.memset(T.rz[:, C * t:C * t + C - M], 0.0))
+
+    def products():
+        mm(0, "us", 0, "x", 0, C)
+        for b in range(3):
+            mm(2 + b, "x", 128 * b, "u", 0, 128)
+        mm(1, "uh", 0, "x", 0, C)
+        mm(5, "us", 0, "x", 0, C)
+        for b in range(3):
+            act(["ps%d" % (2 + b)], [("hs", b, b + 1)], T.hs[:, b:b + 1], T["ps%d" % (2 + b)][:, 1:2])
+        for b in range(3):
+            act(["ps1", ("hs", b, b + 1)], [("sgn", C * b, C * b + C)], pl(T.sgn, b), T.ps1[:, 0:C], SIGN, bias=T.hs[:, b:b + 1], scale=-1.0)
+        for t, bank in enumerate((6, 7, 2, 1)):
+            mm(bank, "k", 128 * (EB0 + t), "x", 0, C)
+        for t, bank in enumerate((6, 7, 2, 1)):
+            act(["ps%d" % bank], ["fp%d" % t], pl(T.fp, t), T["ps%d" % bank][:, 0:C])
+
+    def turning():
+        for name, op, bank in (("le", LE, 3), ("ge", GE, 4)):
+            for b in range(3):
+                vts([("sgn", C * b, C * b + C)], [name + "#%d" % b], T[name][:, b:4 * C:4], pl(T.sgn, b), 0.0, None, op)
+                yield
+            quant(name, name, 0, C, [name + "#%d" % b for b in range(3)] + [name])
+            mm(bank, "k", 128 * K512, name, 0, C)
+            yield
+        vtt(["ps3", "crow"], ["ka"], T.ka[:], T.ps3[:, 0:C], T.crow[:], ADD)
+        yield
+        for m in range(7):
+            even = m % 2 == 0
+            key = T.ka[:] if even else T.win[:, 7 * C:8 * C]
+            last = T.ones[:] if m == 0 else T.mk[:, mark:mark + 4 * (C - 1) + 1:4]
+            scan(["ka" if even else ("win", 7 * C, 8 * C), "ones" if m == 0 else "mk#%d" % (m - 1)], [("win", C * m, C * m + C)],
+                 pl(T.win, m), last, key, MUL, MAX)
+            yield
+            if m == 0:
+                vtt(["ps4", "crow"], [("win", 7 * C, 8 * C)], pl(T.win, 7), T.ps4[:, 0:C], T.crow[:], ADD)
+                yield
+            mark = m if m < 4 else 4 * C + m - 4
+            bank = 3 if even else 4
+            vtt(["ps%d" % bank, ("win", C * m, C * m + C)], ["mk#%d" % m], T.mk[:, mark:mark + 4 * (C - 1) + 1:4],
+                pl(T.win, m), T["ps%d" % bank][:, 0:C], GE)
+            yield
+            if m == 3:
+                quant("mk", "mk", 0, C, ["mk#%d" % i for i in range(4)])
+                mm(6, "k", 128 * K3, "mk", 0, C, True, False)
+                yield
+        quant("mk", "mk", C, 2 * C, ["mk#%d" % i for i in range(4, 7)] + ["mk"])
+        mm(6, "k", 128 * K3, "mk", C, 2 * C, False, True)
+        yield
+        yield
+        vtt(["ps6", "mask"], ["km"], T.km[:], T.ps6[:, 0:C], T.mask[:, 0:C], MUL)
+        yield
+        scan(["km", "foldb"], ["kf"], T.kf[:], T.foldb[:], T.km[:], MUL, ADD)
+        yield
+        for i in range(2):
+            vtt(["kf", ("jg", 24 * i, 24 * i + 24)], [("u1", 24 * i, 24 * i + 24)], T.u1[:, 24 * i:24 * i + 24], T.kf[:, 15:C:16],
+                T.jg[:, 24 * i:24 * i + 24], ADD)
+            yield
+        vtt(["u1", "jt"], ["u2"], T.u2[:], T.u1[:], T.jt[:], MAX)
+        yield
+        vcp(["u2"], ["oab"], T.oab[:], T.u2[:])
+        yield
+        vtt(["win", "oab", "mask"], ["ab"], T.ab[:], T.win[:, 0:8 * C].indirect(T.oab[:, 0:48]), T.mask[:], MUL)
+        yield
+        fold("ab", "abf", 2 * C)
+        yield
+        vcp(["abf"], ["ti"], T.ti[:], T.abf[:, 15:2 * C:16])
+        yield
+        vts(["ti"], ["ti2"], T.ti2[:], T.ti[:], 511, None, AluOpType.bitwise_and)
+        yield
+        vcp(["ti2"], ["at"], T.at[:], T.ti2[:])
+        yield
+
+    def orders():
+        vtt(["ps0", "mask"], ["sm"], T.sm[:], T.ps0[:, 0:C], T.mask[:, 0:C], MUL)
+        yield
+        vtt(["ps0", "mbig"], ["smk"], T.smk[:], T.ps0[:, 0:C], T.mbig[:], MIN)
+        yield
+        fold("sm", "sf", C)
+        vts(["sf"], ["ns"], T.ns[:], T.sf[:, 15:C:16], -1.0, None, MUL)
+        yield
+        score = [T.sf[:, 16 * c + 15:16 * c + 16] for c in range(24)]
+        for c in range(23, 4 * FIRST - 1, -1):
+            i, t = c // 4, c % 4
+            name, a, t8 = "cmp%d" % i, C * (c % 8), c % 8
+            vts(["smk", "sf"], ["sig#%d" % t8], T.sig[:, a + 16 * c:a + 16 * c + 16], T.smk[:, 16 * c:16 * c + 16], score[c], -1.0, GE, ADD)
+            act(["ps5", "ns"], ["sih#%d" % t8], T.sig[:, a:a + 16 * c], T.ps5[:, 0:16 * c], SIGN, bias=T.ns[:, c:c + 1])
+            act(["sig#%d" % t8, "sih#%d" % t8, "half", name], [name + "#%d" % t, ("rs", c, c + 1)], T[name][:, t:64 * c + 60 + t + 1:4],
+                T.sig[:, a:a + 16 * c + 16], SIGN, bias=T.half[:, 0:1], accum_out=T.rs[:, c:c + 1])
+            yield
+        for t in range(4):
+            act(["fp%d" % t, "cl"], ["fc%d" % t], pl(T.fc, t), pl(T.fp, t).indirect(T.cl[:, 0:24]))
+
+        def counts(i):
+            mm(2, "k", 128 * (SGH if i >= FIRST else SG), "cmp%d" % i, 0, WIDE[i], i == 5, i == FIRST)
+
+        def pack(i):
+            name = "cmp%d" % i
+            quant(name, name, 0, WIDE[i], [name + "#%d" % t for t in range(4)] + [name])
+
+        for i in range(FIRST - 1, -1, -1):
+            name = "cmp%d" % i
+            for t in range(3, -1, -1):
+                c = 4 * i + t
+                part = name + "#%d" % t
+                if c:
+                    vts(["ps0", "sf", name], [part], T[name][:, t:64 * (c - 1) + 60 + t + 1:4], T.ps0[:, 0:16 * c], score[c], None, GE)
+                    yield
+                vts(["smk", "sf", name], [part], T[name][:, 64 * c + t:64 * c + 60 + t + 1:4], T.smk[:, 16 * c:16 * c + 16], score[c], None, GE)
+                act([part], [("junk", C * t, C * t + C), ("rs", c, c + 1)], T.junk[:, C * t:C * t + 16 * c + 16], T[name][:, t:64 * c + 60 + t + 1:4],
+                    accum_out=T.rs[:, c:c + 1])
+                yield
+            pack(i)
+            yield
+        for i in range(5, FIRST - 1, -1):
+            pack(i)
+            counts(i)
+            if i == 5:
+                for i2 in range(FIRST):
+                    counts(i2)
+            yield
+        vts([("rs", 4 * FIRST, 24)], [("rs", 4 * FIRST, 24)], T.rs[:, 4 * FIRST:24], T.rs[:, 4 * FIRST:24], 0.5, None, MUL)
+        yield
+        vtt(["rs", "ct0"], ["rc"], T.rc[:], T.rs[:], T.ct0[:], ADD)
+        yield
+        vtt(["ps2", "mask"], ["cm"], T.cm[:], T.ps2[:, 0:C], T.mask[:, 0:C], MUL)
+        yield
+        fold("cm", "cf2", C)
+        yield
+        vtt(["rc", "cf2"], ["posf"], T.posf[:], T.rc[:], T.cf2[:, 15:C:16], SUB)
+        yield
+        vcp(["posf"], ["pos"], T.pos[:], T.posf[:])
+        yield
+        vcp(["iotaj", "pos"], ["inv"], T.inv[:, 0:C].indirect(T.pos[:, 0:24]), T.iotaj[:])
+        yield
+        vtt(["inv", "mask"], ["lm"], T.lm[:], T.inv[:, 0:M], T.mask[:, 0:M], MUL)
+        yield
+        fold("lm", "lf", M)
+        yield
+        vcp(["lf"], ["lo"], T.lo[:], T.lf[:, 15:M:16])
+        yield
+
+    nxt = T.cores[(rank + 1) % len(T.cores)]
+    rid, pid = topo.addr(nxt)[:2]
+    engines = len(topo.engines(core, nxt))
+
+    for r in range(ROUNDS):
+        products()
+        chains = [[orders(), 54, 0], [turning(), 44, 0]]
+        for _ in range(7):
+            next(chains[0][0])
+        if r == 0:
+            tables()
+        while chains:
+            c = min(chains, key=lambda e: e[2] / e[1])
+            c[2] += 1
+            if next(c[0], 0) == 0:
+                chains.remove(c)
+        for t in range(4):
+            act(["fc%d" % t, "at"], ["ag%d" % t], pl(T.ag, t), pl(T.fc, t).indirect(T.at[:, 0:24]))
+            vtt(["fc%d" % t, "at", "ag%d" % t], ["zp%d" % t], pl(T.zp, t), pl(T.fc, t).indirect(T.at[:, 24:48]), pl(T.ag, t), ADD)
+        for t in range(4):
+            out, in_ = T.eb[:, t:4 * M:4], pl(T.zp, t).indirect(T.lo[:, 0:10])
+            if t < 2:
+                act(["zp%d" % t, "lo"], ["eb#%d" % t], out, in_)
+            else:
+                vcp(["zp%d" % t, "lo"], ["eb#%d" % t], out, in_)
+        name, land, arr = "e%d" % r, "land%d" % r, "arr%d" % r
+        quant(name, "eb", 0, M, ["eb#%d" % t for t in range(4)])
+        waits("p", full([name + "_q"]), [])
+        g.remote_dma(T[land + "_q"][:, 0:M].bitcast(dt.uint8), T[name + "_q"][:, 0:M].bitcast(dt.uint8), T.sem[arr], T.sem.sent, pid, rid,
+                     topo.mask(core, nxt))
+        g.remote_dma(T[land + "_s"][:, 0:M], T[name + "_s"][:, 0:M], T.sem[arr], T.sem.sent, pid, rid, topo.mask(core, nxt))
+        note("d" + arr, (arr, 2 * engines), [], full([land + "_q"]))
+        for a, b, c in ((0, 224, 384), (160, 160, 224), (224, 0, 160)):
+            act(["inv"], [("wrow", a, a + c - b)], T.wrow[:, a:a + c - b], T.inv[:, b:c])
+        vcp(["wrow", "pos"], ["swap"], T.swap[:], T.wrow[:, 0:C].indirect(T.pos[:, 0:24]))
+        if r + 1 < ROUNDS:
+            vtt(["swap", "cl", "mask"], ["crm"], T.crm[:], T.swap[:, 0:C].indirect(T.cl[:, 0:24]), T.mask[:, 0:C], MUL)
+            fold("crm", "crf", C)
+            vcp(["crf"], ["cl"], T.cl[:], T.crf[:, 15:C:16])
+        else:
+            vcp(["swap", "cl"], ["crm"], T.crm[:], T.swap[:, 0:C].indirect(T.cl[:, 0:24]))
+            dma("y", "stp", ["crm"], [], T.op[:], T.crm[0:128:16, :])
+        if r == 0:
+            quant("v", "vb")
+        banks = (1, 2, 6, 7)
+        for b in range(4):
+            run("t", ["w_q", "w_s", land + "_q"], ["ps%d" % banks[b]],
+                lambda: g.tensor.matmul_mx(T["ps%d" % banks[b]][:, 0:M], codes("w", 128 * b, 128 * b + 128), plane("w", 128 * b, 128 * b + 128),
+                                           codes(land, 0, M), plane(land, 0, M), True, True))
+        for b in range(4):
+            out, in_ = T.rz[:, C * b + C - M:C * b + C], T["ps%d" % banks[b]][:, 0:M]
+            if b % 2 == 0:
+                vts(["ps%d" % banks[b]], [("rz%d" % b, C - M, C)], out, in_, 0.03125, None, MUL)
+            else:
+                act(["ps%d" % banks[b]], [("rz%d" % b, C - M, C)], out, in_, scale=0.03125)
+        for b in range(4):
+            vtt(["rz%d" % b, "pos", "zp%d" % b], ["xb#%d" % b], T.xb[:, b:4 * C:4], pl(T.rz, b).indirect(T.pos[:, 0:24]), pl(T.zp, b), ADD)
+        quant("x", "xb", 0, C, ["xb#%d" % b for b in range(4)])
+
+    mm(0, "v", 0, "x", 0, C)
+    dma("y", "stc", ["x_q"], [], T.oc[:], T.x_q[:, 0:C].bitcast(dt.uint8))
+    for k in range(4):
+        dma("y", "sts%d" % k, ["x_q"], [], T.osc[4 * k:4 * k + 4, :], T.x_s[32 * k:32 * k + 4, 0:C])
+    act(["ps0"], ["yb"], T.yb[:], T.ps0[:, 0:C])
+    dma("s", "sty", ["yb"], [], T.y[:], T.yb[:])
+    for s in ("vec", "act", "ten", "pool"):
+        g.wait_ge(T.sem[s], count[s])
+    for s in ("ldx", "ldu", "ldv", "ldw", "lds", "ldc", "sty", "stp", "stc", "sts0", "sts1", "sts2", "sts3"):
+        g.wait_ge(T.sem[s], 16)
+    g.wait_ge(T.sem.sent, 2 * engines * ROUNDS)

@@ -1,7 +1,7 @@
 from concourse.mybir import dt, AluOpType, ActivationFunctionType
 
 C, M, ROUNDS = 384, 160, 3
-FIRST = 4
+FIRST = 3
 WIDE = [max(128, 64 * (i + 1)) for i in range(6)]
 X4 = "float8_e4m3fn_x4"
 F32, BF = "float32", "bfloat16"
@@ -17,25 +17,25 @@ def _pair(name, cols):
     _buf(name + "_s", cols, "uint8")
 
 
-for _n, _c in (("xb", 4 * C), ("ub", 512), ("vb", 512), ("cb", 8 * 512), ("sig", 8 * C), ("sgn", 3 * C), ("le", 4 * C),
-               ("ge", 4 * C), ("mk", 8 * C), ("junk", 4 * C), ("eb", 4 * M), ("ones", C), ("km", C), ("kf", C), ("foldb", C)):
+for _n, _c in (("xb", 4 * C), ("ub", 512), ("vb", 512), ("cb", 8 * 512), ("sig", 12 * C), ("hb", 512), ("dg", 4 * C), ("dr", C),
+               ("sgn", 3 * C), ("le", 4 * C), ("ge", 4 * C), ("mk", 8 * C), ("junk", 4 * C), ("eb", 4 * M), ("ones", C),
+               ("km", C), ("kf", C), ("foldb", C)):
     _buf(_n, _c, BF)
 for _n, _c in (("fp", BF), ("fc", BF), ("ag", BF), ("zp", BF), ("rz", F32)):
     _buf(_n, 4 * C, _c)
 for _i in range(6):
     _buf("cmp%d" % _i, 4 * WIDE[_i], BF)
-for _n, _c in (("iotaj", C), ("crow", C), ("jmod", 2 * C), ("g8", 512), ("e4", 512), ("jt", 48), ("jg", 48), ("ct0", 24),
-               ("qg", 8), ("mask", 2 * C), ("fold0", 2 * C), ("mbig", C), ("hs", 4), ("ka", C), ("win", 8 * C), ("u1", 48),
-               ("u2", 48), ("ab", 2 * C), ("abf", 2 * C), ("sm", C), ("sf", C), ("smk", C), ("rs", 24), ("ns", 24),
-               ("half", 4), ("rc", 24), ("cm", C), ("cf2", C), ("posf", 24), ("inv", C), ("lm", M), ("lf", M), ("wrow", C),
-               ("swap", C), ("crm", C), ("crf", C), ("yb", C)):
+for _n, _c in (("iotaj", C), ("crow", C), ("jmod", C), ("g8", 512), ("ex", C), ("jt", 48), ("jg", 48), ("ct0", 24), ("qg", 8),
+               ("mask", C), ("fold0", C), ("mbig", C), ("hs", 4), ("ka", C), ("win", 8 * C), ("u1", 48), ("ab", 2 * C),
+               ("abf", 2 * C), ("sm", C), ("sf", C), ("smk", C), ("rs", 24), ("ns", 24), ("half", 4), ("rc", 24), ("cm", C),
+               ("cf2", C), ("inv", C), ("wrow", C), ("swap", C), ("crm", C), ("crf", C), ("yb", C)):
     _buf(_n, _c, F32)
-for _n, _c in (("cfi", 24), ("pcol", 4), ("us32", 8), ("ti", 48), ("ti2", 48)):
+for _n, _c in (("cfi", 24), ("pcol", 4), ("us32", 32), ("ti", 48)):
     _buf(_n, _c, "int32")
-for _n, _c in (("uso", 8), ("uho", 8), ("oab", 48), ("at", 48), ("pos", 24), ("lo", 10), ("cl", 24)):
+for _n, _c in (("uso", 32), ("uho", 8), ("oab", 48), ("at", 48), ("pos", 24), ("lo", 10), ("cl", 24)):
     _buf(_n, _c, "uint16")
 for _n, _c in (("u", 128), ("us", 128), ("uh", 128), ("v", 128), ("w", 512), ("x", C), ("k", 8 * 128), ("le", C), ("ge", C),
-               ("mk", 2 * C)):
+               ("mk", 2 * C), ("dg", C)):
     _pair(_n, _c)
 for _i in range(6):
     _pair("cmp%d" % _i, WIDE[_i])
@@ -44,14 +44,14 @@ for _r in range(ROUNDS):
     _pair("land%d" % _r, M)
 for _b in range(8):
     _buf("ps%d" % _b, 512, F32, "psum")
-SEMAPHORES = ["vec", "act", "ten", "pool", "sent", "ldx", "ldu", "ldv", "ldw", "lds", "ldc", "sty", "stp", "stc",
+SEMAPHORES = ["vec", "act", "ten", "pool", "sent", "ldx", "ldu", "ldv", "ldw", "lds", "ldc", "sty", "sty2", "stp", "stc",
               "sts0", "sts1", "sts2", "sts3", "arr0", "arr1", "arr2"]
 
 LT, LE, GE, EQ = AluOpType.is_lt, AluOpType.is_le, AluOpType.is_ge, AluOpType.is_equal
 ADD, SUB, MUL, MAX, MIN = AluOpType.add, AluOpType.subtract, AluOpType.mult, AluOpType.max, AluOpType.min
 COPY, SIGN = ActivationFunctionType.Copy, ActivationFunctionType.Sign
 ABS, RELU = ActivationFunctionType.Abs, ActivationFunctionType.Relu
-EB0, SG, K512, K3, SGH = 0, 4, 5, 6, 7
+EB0, K512, K3, SG, SGH = 0, 4, 5, 6, 7
 
 
 def rank_program(g, core, T, topo):
@@ -174,14 +174,17 @@ def rank_program(g, core, T, topo):
 
     ok = {"allow_small_or_imprecise_dtypes": True}
     iota("us32", 0, 8, [[16, 8]], 0, 0)
+    iota("us32", 8, 32, [[16, 24]], 15, 0)
     iota("pcol", 0, 1, [[1, 1]], 0, 1)
-    iota("jmod", 0, 2 * C, [[0, 48], [1, 16]], 0, 0, **ok)
-    iota("g8", 0, 512, [[1, 8], [0, 64]], 0, 0, **ok)
-    iota("e4", 0, 512, [[1, 512]], 0, -4, **ok)
-    iota("crow", 0, C, [[1, C]], -512, 0, **ok)
+    iota("jmod", 0, C, [[0, 24], [1, 16]], 0, 0, **ok)
     iota("jt", 0, 24, [[16, 24]], 0, 0, **ok)
     iota("jt", 24, 48, [[16, 24]], 0, 0, **ok)
-    for i in (5, 4, 3, 2, 1, 0):
+    fill("hb", 0, 512, 0.5)
+    for t in range(4):
+        run("p", ["hb"], [tile(EB0 + t)], lambda: P.affine_select(const(EB0 + t), T.hb[:], [[1, 512]], EQ, 0.0, -t, -4))
+    iota("g8", 0, 512, [[1, 8], [0, 64]], 0, 0, **ok)
+    iota("crow", 0, C, [[1, C]], -512, 0, **ok)
+    for i in (4, 3, 1, 0):
         iota("cmp%d" % i, 256 * i, 4 * WIDE[i], [[0, 4 * WIDE[i] - 256 * i]], 0, 0, **ok)
     iota("iotaj", 0, C, [[1, C]], 0, 0, **ok)
 
@@ -197,31 +200,45 @@ def rank_program(g, core, T, topo):
     vts([("qg", 0, 2)], [("qg", 4, 6)], T.qg[:, 4:6], T.qg[:, 0:2], -1.0, None, MUL)
     q_of, g_of = T.qg[:, 0:1], T.qg[:, 1:2]
     act(["jmod"], ["fold0"], T.fold0[:], T.jmod[:], SIGN)
-    act(["jmod"], ["foldb"], T.foldb[:], T.jmod[:, 0:C], SIGN)
+    act(["jmod"], ["foldb"], T.foldb[:], T.jmod[:], SIGN)
     act(["jmod", ("qg", 4, 6)], ["mask"], T.mask[:], T.jmod[:], ABS, bias=T.qg[:, 4:5])
     act(["mask"], ["mask"], T.mask[:], T.mask[:], RELU, bias=1.0, scale=-1.0)
-    act(["g8", ("qg", 4, 6)], ["g8"], T.g8[:], T.g8[:], ABS, bias=T.qg[:, 5:6])
-    act(["g8"], [tile(SG)], const(SG), T.g8[:], RELU, bias=1.0, scale=-1.0)
-    act(["g8"], [tile(SGH)], const(SGH), T.g8[:], RELU, bias=0.5, scale=-0.5)
+
+    def blank(name, first):
+        act(["jmod"], [name], T[name][:, first:first + 4 * C - 3:4], T.jmod[:], scale=0.0)
+
+    blank("le", 3)
+    blank("ge", 3)
+    for i in (5, 2):
+        fill("cmp%d" % i, 256 * i, 4 * WIDE[i], 0.0)
+    fill("dg", 0, 4 * C, 0.0)
     quant("u", "ub")
-    for name, off in (("us", "uso"), ("uh", "uho")):
+
+    def repeat(name, off):
+        run("v", ["u_q", off], [name + "_s"], lambda: V.tensor_copy(T[name + "_s"][:, 0:128], T.u_s[:, 0:128].indirect(T[off][:, 0:8])))
         run("v", ["u_q", off], [name + "_q"],
             lambda: V.tensor_copy(T[name + "_q"][:, 0:128].bitcast(dt.uint32), T.u_q[:, 0:128].bitcast(dt.uint32).indirect(T[off][:, 0:8])))
-        run("v", ["u_q", off], [name + "_q"],
-            lambda: V.tensor_copy(T[name + "_s"][:, 0:128], T.u_s[:, 0:128].indirect(T[off][:, 0:8])))
+
+    repeat("us", "uso")
     quant("x", "xb")
-    vts(["jmod", ("qg", 0, 2)], ["mbig"], T.mbig[:], T.jmod[:, 0:C], q_of, 2e29, LT, MUL)
-    for t in range(4):
-        vts(["e4"], [tile(EB0 + t)], const(EB0 + t), T.e4[:], float(t), 0.5, EQ, MUL)
+    repeat("uh", "uho")
+    vts(["jmod", ("qg", 0, 2)], ["mbig"], T.mbig[:], T.jmod[:], q_of, 2e29, LT, MUL)
+    fill("rs", 0, 1, 0.0)
     vts(["mbig"], ["mbig"], T.mbig[:], T.mbig[:], 1e29, None, SUB)
-    quant("k", "cb", 0, 512, [("cb", 0, 2048)])
-    quant("k", "cb", 512, 1024, [("cb", 2048, 4096)])
-    for name, first in (("le", 3), ("ge", 3), ("mk", 4 * C + 3)):
-        run("v", [], [name], lambda: V.memset(T[name][:, first:first + 4 * C - 3:4], 0.0))
-    vcp(["cfi"], ["cl"], T.cl[:], T.cfi[:])
+
+    def packs():
+        quant("k", "cb", 512, 768, [("cb", 2048, 3072)])
+        quant("k", "cb", 0, 512, [("cb", 0, 2048)])
+        vcp(["cfi"], ["cl"], T.cl[:], T.cfi[:])
+        act(["g8", ("qg", 4, 6)], ["g8"], T.g8[:], T.g8[:], ABS, bias=T.qg[:, 5:6])
+        act(["g8"], [tile(SG)], const(SG), T.g8[:], RELU, bias=1.0, scale=-1.0)
+        act(["g8"], [tile(SGH)], const(SGH), T.g8[:], RELU, bias=0.5, scale=-0.5)
 
     def tables():
         lead = 4 * FIRST
+        blank("mk", 4 * C + 3)
+        for t in range(4):
+            act(["jmod"], [("rz%d" % t, 0, C - M)], T.rz[:, C * t:C * t + C - M], T.jmod[:, 0:C - M], scale=0.0)
         vts(["jt", ("qg", 0, 2)], ["jt"], T.jt[:], T.jt[:], q_of, None, ADD)
         vts([("qg", 0, 2)], [("qg", 2, 3)], T.qg[:, 2:3], g_of, 384.0, None, MUL)
         vts([("qg", 0, 2)], [("qg", 3, 4)], T.qg[:, 3:4], g_of, 384.0, 384.0, MUL, ADD)
@@ -230,8 +247,6 @@ def rank_program(g, core, T, topo):
         vts(["jt"], [("ct0", 0, lead)], T.ct0[:, 0:lead], T.jt[:, 0:lead], -1.0, 383.0 - 8 * (24 - lead), MUL, ADD)
         vts(["jt", ("qg", 0, 2)], [("ct0", lead, 24)], T.ct0[:, lead:24], T.jt[:, lead:24], 0.0, q_of, MUL, SUB)
         vts([("ct0", lead, 24)], [("ct0", lead, 24)], T.ct0[:, lead:24], T.ct0[:, lead:24], 199.0, None, ADD)
-        for t in range(4):
-            run("v", [], [("rz%d" % t, 0, C - M)], lambda: V.memset(T.rz[:, C * t:C * t + C - M], 0.0))
 
     def products():
         mm(0, "us", 0, "x", 0, C)
@@ -243,6 +258,8 @@ def rank_program(g, core, T, topo):
             act(["ps%d" % (2 + b)], [("hs", b, b + 1)], T.hs[:, b:b + 1], T["ps%d" % (2 + b)][:, 1:2])
         for b in range(3):
             act(["ps1", ("hs", b, b + 1)], [("sgn", C * b, C * b + C)], pl(T.sgn, b), T.ps1[:, 0:C], SIGN, bias=T.hs[:, b:b + 1], scale=-1.0)
+
+    def planes():
         for t, bank in enumerate((6, 7, 2, 1)):
             mm(bank, "k", 128 * (EB0 + t), "x", 0, C)
         for t, bank in enumerate((6, 7, 2, 1)):
@@ -281,96 +298,117 @@ def rank_program(g, core, T, topo):
         mm(6, "k", 128 * K3, "mk", C, 2 * C, False, True)
         yield
         yield
-        vtt(["ps6", "mask"], ["km"], T.km[:], T.ps6[:, 0:C], T.mask[:, 0:C], MUL)
+        vtt(["ps6", "mask"], ["km"], T.km[:], T.ps6[:, 0:C], T.mask[:], MUL)
         yield
         scan(["km", "foldb"], ["kf"], T.kf[:], T.foldb[:], T.km[:], MUL, ADD)
         yield
         for i in range(2):
-            vtt(["kf", ("jg", 24 * i, 24 * i + 24)], [("u1", 24 * i, 24 * i + 24)], T.u1[:, 24 * i:24 * i + 24], T.kf[:, 15:C:16],
-                T.jg[:, 24 * i:24 * i + 24], ADD)
+            a, b = 24 * i, 24 * i + 24
+            vtt(["kf", ("jg", a, b)], [("u1", a, b)], T.u1[:, a:b], T.kf[:, 15:C:16], T.jg[:, a:b], ADD)
             yield
-        vtt(["u1", "jt"], ["u2"], T.u2[:], T.u1[:], T.jt[:], MAX)
+        vtt(["u1", "jt"], ["u1"], T.u1[:], T.u1[:], T.jt[:], MAX)
         yield
-        vcp(["u2"], ["oab"], T.oab[:], T.u2[:])
+        vcp(["u1"], ["oab"], T.oab[:], T.u1[:])
         yield
-        vtt(["win", "oab", "mask"], ["ab"], T.ab[:], T.win[:, 0:8 * C].indirect(T.oab[:, 0:48]), T.mask[:], MUL)
-        yield
-        fold("ab", "abf", 2 * C)
-        yield
-        vcp(["abf"], ["ti"], T.ti[:], T.abf[:, 15:2 * C:16])
-        yield
-        vts(["ti"], ["ti2"], T.ti2[:], T.ti[:], 511, None, AluOpType.bitwise_and)
-        yield
-        vcp(["ti2"], ["at"], T.at[:], T.ti2[:])
-        yield
+        for i in range(2):
+            a, b, ab, abf = 24 * i, 24 * i + 24, ("ab", C * i, C * i + C), ("abf", C * i, C * i + C)
+            vtt(["win", "oab", "mask"], [ab], pl(T.ab, i), T.win[:, 0:8 * C].indirect(T.oab[:, a:b]), T.mask[:], MUL)
+            yield
+            scan([ab, "fold0"], [abf], pl(T.abf, i), T.fold0[:], pl(T.ab, i), MUL, ADD)
+            yield
+            vcp([abf], [("ti", a, b)], T.ti[:, a:b], T.abf[:, C * i + 15:C * i + C:16])
+            yield
+            vts([("ti", a, b)], [("ti", a, b)], T.ti[:, a:b], T.ti[:, a:b], 511, None, AluOpType.bitwise_and)
+            yield
+            vcp([("ti", a, b)], [("at", a, b)], T.at[:, a:b], T.ti[:, a:b])
+            if i == 0:
+                for t in range(4):
+                    act(["fc%d" % t, ("at", a, b)], ["ag%d" % t], pl(T.ag, t), pl(T.fc, t).indirect(T.at[:, a:b]))
+            yield
 
-    def orders():
-        vtt(["ps0", "mask"], ["sm"], T.sm[:], T.ps0[:, 0:C], T.mask[:, 0:C], MUL)
+    def orders(r):
+        vtt(["ps0", "mask"], ["sm"], T.sm[:], T.ps0[:, 0:C], T.mask[:], MUL)
         yield
         vtt(["ps0", "mbig"], ["smk"], T.smk[:], T.ps0[:, 0:C], T.mbig[:], MIN)
         yield
         fold("sm", "sf", C)
         vts(["sf"], ["ns"], T.ns[:], T.sf[:, 15:C:16], -1.0, None, MUL)
+        act(["sf", "uso"], ["ex"], T.ex[:], T.sf[:, 0:C].indirect(T.uso[:, 8:32]))
         yield
         score = [T.sf[:, 16 * c + 15:16 * c + 16] for c in range(24)]
-        for c in range(23, 4 * FIRST - 1, -1):
-            i, t = c // 4, c % 4
-            name, a, t8 = "cmp%d" % i, C * (c % 8), c % 8
-            vts(["smk", "sf"], ["sig#%d" % t8], T.sig[:, a + 16 * c:a + 16 * c + 16], T.smk[:, 16 * c:16 * c + 16], score[c], -1.0, GE, ADD)
-            act(["ps5", "ns"], ["sih#%d" % t8], T.sig[:, a:a + 16 * c], T.ps5[:, 0:16 * c], SIGN, bias=T.ns[:, c:c + 1])
-            act(["sig#%d" % t8, "sih#%d" % t8, "half", name], [name + "#%d" % t, ("rs", c, c + 1)], T[name][:, t:64 * c + 60 + t + 1:4],
-                T.sig[:, a:a + 16 * c + 16], SIGN, bias=T.half[:, 0:1], accum_out=T.rs[:, c:c + 1])
-            yield
-        for t in range(4):
-            act(["fp%d" % t, "cl"], ["fc%d" % t], pl(T.fc, t), pl(T.fp, t).indirect(T.cl[:, 0:24]))
+        for c in range(23, 4 * FIRST - 2, -1):
+            if c >= 4 * FIRST:
+                a = C * (c % 12)
+                act(["ps5", "ns"], [("sig", a, a + C)], T.sig[:, a:a + 16 * c], T.ps5[:, 0:16 * c], SIGN, bias=T.ns[:, c:c + 1])
+            if c < 23:
+                d = c + 1
+                i, t, a = d // 4, d % 4, C * (d % 12)
+                name = "cmp%d" % i
+                act([("sig", a, a + C), "half", name], [name + "#%d" % t, ("rs", d, d + 1)], T[name][:, t:64 * (d - 1) + 60 + t + 1:4],
+                    T.sig[:, a:a + 16 * d], SIGN, bias=T.half[:, 0:1], accum_out=T.rs[:, d:d + 1])
+                if d == 20:
+                    yield
 
-        def counts(i):
-            mm(2, "k", 128 * (SGH if i >= FIRST else SG), "cmp%d" % i, 0, WIDE[i], i == 5, i == FIRST)
+        def counts(name, half, cols, first=False, last=False):
+            mm(2, "k", 128 * (SGH if half else SG), name, 0, cols, first, last)
 
         def pack(i):
             name = "cmp%d" % i
             quant(name, name, 0, WIDE[i], [name + "#%d" % t for t in range(4)] + [name])
+            counts(name, i >= FIRST, WIDE[i], i == 5, i == FIRST)
 
         for i in range(FIRST - 1, -1, -1):
             name = "cmp%d" % i
             for t in range(3, -1, -1):
                 c = 4 * i + t
-                part = name + "#%d" % t
                 if c:
-                    vts(["ps0", "sf", name], [part], T[name][:, t:64 * (c - 1) + 60 + t + 1:4], T.ps0[:, 0:16 * c], score[c], None, GE)
+                    part, end = name + "#%d" % t, 64 * (c - 1) + 60 + t + 1
+                    vts(["ps0", "sf", name], [part], T[name][:, t:end:4], T.ps0[:, 0:16 * c], score[c], None, GE)
+                    act([part], [("junk", C * t, C * t + C), ("rs", c, c + 1)], T.junk[:, C * t:C * t + 16 * c], T[name][:, t:end:4],
+                        accum_out=T.rs[:, c:c + 1])
                     yield
-                vts(["smk", "sf", name], [part], T[name][:, 64 * c + t:64 * c + 60 + t + 1:4], T.smk[:, 16 * c:16 * c + 16], score[c], None, GE)
-                act([part], [("junk", C * t, C * t + C), ("rs", c, c + 1)], T.junk[:, C * t:C * t + 16 * c + 16], T[name][:, t:64 * c + 60 + t + 1:4],
-                    accum_out=T.rs[:, c:c + 1])
+            if i == FIRST - 1:
+                vtt(["smk", "ex", "dg"], ["dg#0"], T.dg[:, 0:4 * C - 3:4], T.smk[:], T.ex[:], GE)
                 yield
+        if r == 0:
+            quant("k", "cb", 768, 1024, [("cb", 3072, 4096)])
+            yield
+        pack(5)
+        yield
+        quant("dg", "dg", 0, C, ["dg#0", "dg"])
+        counts("dg", False, C)
+        yield
+        scan(["dg#0", "foldb"], ["dr"], T.dr[:], T.foldb[:], T.dg[:, 0:4 * C - 3:4], MUL, ADD)
+        yield
+        vtt(["ct0", "dr"], ["rc"], T.rc[:], T.ct0[:], T.dr[:, 15:C:16], ADD)
+        yield
+        for i in range(FIRST - 1, -1, -1):
             pack(i)
             yield
-        for i in range(5, FIRST - 1, -1):
+        for t in range(4):
+            act(["fp%d" % t, "cl"], ["fc%d" % t], pl(T.fc, t), pl(T.fp, t).indirect(T.cl[:, 0:24]))
+        for i in range(4, FIRST - 1, -1):
             pack(i)
-            counts(i)
-            if i == 5:
-                for i2 in range(FIRST):
-                    counts(i2)
             yield
         vts([("rs", 4 * FIRST, 24)], [("rs", 4 * FIRST, 24)], T.rs[:, 4 * FIRST:24], T.rs[:, 4 * FIRST:24], 0.5, None, MUL)
         yield
-        vtt(["rs", "ct0"], ["rc"], T.rc[:], T.rs[:], T.ct0[:], ADD)
+        vtt(["rs", "rc"], ["rc"], T.rc[:], T.rs[:], T.rc[:], ADD)
         yield
-        vtt(["ps2", "mask"], ["cm"], T.cm[:], T.ps2[:, 0:C], T.mask[:, 0:C], MUL)
+        vtt(["ps2", "mask"], ["cm"], T.cm[:], T.ps2[:, 0:C], T.mask[:], MUL)
         yield
         fold("cm", "cf2", C)
         yield
-        vtt(["rc", "cf2"], ["posf"], T.posf[:], T.rc[:], T.cf2[:, 15:C:16], SUB)
+        vtt(["rc", "cf2"], ["rc"], T.rc[:], T.rc[:], T.cf2[:, 15:C:16], SUB)
         yield
-        vcp(["posf"], ["pos"], T.pos[:], T.posf[:])
+        vcp(["rc"], ["pos"], T.pos[:], T.rc[:])
         yield
         vcp(["iotaj", "pos"], ["inv"], T.inv[:, 0:C].indirect(T.pos[:, 0:24]), T.iotaj[:])
         yield
-        vtt(["inv", "mask"], ["lm"], T.lm[:], T.inv[:, 0:M], T.mask[:, 0:M], MUL)
+        vtt(["inv", "mask"], ["cm"], T.cm[:, 0:M], T.inv[:, 0:M], T.mask[:, 0:M], MUL)
         yield
-        fold("lm", "lf", M)
+        fold("cm", "cf2", M)
         yield
-        vcp(["lf"], ["lo"], T.lo[:], T.lf[:, 15:M:16])
+        vcp(["cf2"], ["lo"], T.lo[:], T.cf2[:, 15:M:16])
         yield
 
     nxt = T.cores[(rank + 1) % len(T.cores)]
@@ -379,9 +417,12 @@ def rank_program(g, core, T, topo):
 
     for r in range(ROUNDS):
         products()
-        chains = [[orders(), 54, 0], [turning(), 44, 0]]
-        for _ in range(7):
+        chains = [[orders(r), 34, 0], [turning(), 48, 0]]
+        for _ in range(4):
             next(chains[0][0])
+        if r == 0:
+            packs()
+        planes()
         if r == 0:
             tables()
         while chains:
@@ -390,8 +431,7 @@ def rank_program(g, core, T, topo):
             if next(c[0], 0) == 0:
                 chains.remove(c)
         for t in range(4):
-            act(["fc%d" % t, "at"], ["ag%d" % t], pl(T.ag, t), pl(T.fc, t).indirect(T.at[:, 0:24]))
-            vtt(["fc%d" % t, "at", "ag%d" % t], ["zp%d" % t], pl(T.zp, t), pl(T.fc, t).indirect(T.at[:, 24:48]), pl(T.ag, t), ADD)
+            vtt(["fc%d" % t, ("at", 24, 48), "ag%d" % t], ["zp%d" % t], pl(T.zp, t), pl(T.fc, t).indirect(T.at[:, 24:48]), pl(T.ag, t), ADD)
         for t in range(4):
             out, in_ = T.eb[:, t:4 * M:4], pl(T.zp, t).indirect(T.lo[:, 0:10])
             if t < 2:
@@ -409,7 +449,7 @@ def rank_program(g, core, T, topo):
             act(["inv"], [("wrow", a, a + c - b)], T.wrow[:, a:a + c - b], T.inv[:, b:c])
         vcp(["wrow", "pos"], ["swap"], T.swap[:], T.wrow[:, 0:C].indirect(T.pos[:, 0:24]))
         if r + 1 < ROUNDS:
-            vtt(["swap", "cl", "mask"], ["crm"], T.crm[:], T.swap[:, 0:C].indirect(T.cl[:, 0:24]), T.mask[:, 0:C], MUL)
+            vtt(["swap", "cl", "mask"], ["crm"], T.crm[:], T.swap[:, 0:C].indirect(T.cl[:, 0:24]), T.mask[:], MUL)
             fold("crm", "crf", C)
             vcp(["crf"], ["cl"], T.cl[:], T.crf[:, 15:C:16])
         else:
@@ -424,7 +464,7 @@ def rank_program(g, core, T, topo):
                                            codes(land, 0, M), plane(land, 0, M), True, True))
         for b in range(4):
             out, in_ = T.rz[:, C * b + C - M:C * b + C], T["ps%d" % banks[b]][:, 0:M]
-            if b % 2 == 0:
+            if b == 0:
                 vts(["ps%d" % banks[b]], [("rz%d" % b, C - M, C)], out, in_, 0.03125, None, MUL)
             else:
                 act(["ps%d" % banks[b]], [("rz%d" % b, C - M, C)], out, in_, scale=0.03125)
@@ -432,14 +472,18 @@ def rank_program(g, core, T, topo):
             vtt(["rz%d" % b, "pos", "zp%d" % b], ["xb#%d" % b], T.xb[:, b:4 * C:4], pl(T.rz, b).indirect(T.pos[:, 0:24]), pl(T.zp, b), ADD)
         quant("x", "xb", 0, C, ["xb#%d" % b for b in range(4)])
 
-    mm(0, "v", 0, "x", 0, C)
+    h = C // 2
+    mm(0, "v", 0, "x", 0, h)
+    mm(5, "v", 0, "x", h, C)
     dma("y", "stc", ["x_q"], [], T.oc[:], T.x_q[:, 0:C].bitcast(dt.uint8))
     for k in range(4):
         dma("y", "sts%d" % k, ["x_q"], [], T.osc[4 * k:4 * k + 4, :], T.x_s[32 * k:32 * k + 4, 0:C])
-    act(["ps0"], ["yb"], T.yb[:], T.ps0[:, 0:C])
-    dma("s", "sty", ["yb"], [], T.y[:], T.yb[:])
+    act(["ps0"], [("yb", 0, h)], T.yb[:, 0:h], T.ps0[:, 0:h])
+    dma("s", "sty", [("yb", 0, h)], [], T.y[:, 0:h], T.yb[:, 0:h])
+    vcp(["ps5"], [("yb", h, C)], T.yb[:, h:C], T.ps5[:, 0:h])
+    dma("s", "sty2", [("yb", h, C)], [], T.y[:, h:C], T.yb[:, h:C])
     for s in ("vec", "act", "ten", "pool"):
         g.wait_ge(T.sem[s], count[s])
-    for s in ("ldx", "ldu", "ldv", "ldw", "lds", "ldc", "sty", "stp", "stc", "sts0", "sts1", "sts2", "sts3"):
+    for s in ("ldx", "ldu", "ldv", "ldw", "lds", "ldc", "sty", "sty2", "stp", "stc", "sts0", "sts1", "sts2", "sts3"):
         g.wait_ge(T.sem[s], 16)
     g.wait_ge(T.sem.sent, 2 * engines * ROUNDS)

@@ -1,6 +1,7 @@
 from concourse.mybir import dt, AluOpType, ActivationFunctionType
 
 C, M, ROUNDS = 384, 160, 3
+HALF = C // 2
 FIRST = 3
 WIDE = [max(128, 64 * (i + 1)) for i in range(6)]
 X4 = "float8_e4m3fn_x4"
@@ -19,16 +20,16 @@ def _pair(name, cols):
 
 for _n, _c in (("xb", 4 * C), ("ub", 512), ("vb", 512), ("cb", 8 * 512), ("sig", 12 * C), ("hb", 512), ("dg", 4 * C), ("dr", C),
                ("sgn", 3 * C), ("le", 4 * C), ("ge", 4 * C), ("mk", 8 * C), ("junk", 4 * C), ("eb", 4 * M), ("ones", C),
-               ("km", C), ("kf", C), ("foldb", C)):
+               ("foldb", C)):
     _buf(_n, _c, BF)
 for _n, _c in (("fp", BF), ("fc", BF), ("ag", BF), ("zp", BF), ("rz", F32)):
     _buf(_n, 4 * C, _c)
 for _i in range(6):
     _buf("cmp%d" % _i, 4 * WIDE[_i], BF)
-for _n, _c in (("iotaj", C), ("crow", C), ("jmod", C), ("g8", 512), ("ex", C), ("jt", 48), ("jg", 48), ("ct0", 24), ("qg", 8),
-               ("mask", C), ("fold0", C), ("mbig", C), ("hs", 4), ("ka", C), ("win", 8 * C), ("u1", 48), ("ab", 2 * C),
-               ("abf", 2 * C), ("sm", C), ("sf", C), ("smk", C), ("rs", 24), ("ns", 24), ("half", 4), ("rc", 24), ("cm", C),
-               ("cf2", C), ("inv", C), ("wrow", C), ("swap", C), ("crm", C), ("crf", C), ("yb", C)):
+for _n, _c in (("iotaj", C), ("crow", C), ("jmod", C), ("g8", 512), ("ex", C), ("jt", 48), ("jg", 48), ("ct0", 24), ("qg", 10),
+               ("mask", C), ("fold0", C), ("pick", C), ("mbig", C), ("hs", 4), ("ka", C), ("win", 8 * C), ("u1", 48), ("kf", C),
+               ("ar", 2 * C), ("abf", 2 * C), ("sm", C), ("sf", C), ("smk", C), ("rs", 24), ("half", 4), ("rc", 24), ("cf2", C),
+               ("inv", C), ("wrow", C), ("swap", C), ("crm", C), ("crf", C), ("yb", C)):
     _buf(_n, _c, F32)
 for _n, _c in (("cfi", 24), ("pcol", 4), ("us32", 32), ("ti", 48)):
     _buf(_n, _c, "int32")
@@ -47,10 +48,11 @@ for _b in range(8):
 SEMAPHORES = ["vec", "act", "ten", "pool", "sent", "ldx", "ldu", "ldv", "ldw", "lds", "ldc", "sty", "sty2", "stp", "stc",
               "sts0", "sts1", "sts2", "sts3", "arr0", "arr1", "arr2"]
 
-LT, LE, GE, EQ = AluOpType.is_lt, AluOpType.is_le, AluOpType.is_ge, AluOpType.is_equal
+LE, GE, EQ = AluOpType.is_le, AluOpType.is_ge, AluOpType.is_equal
 ADD, SUB, MUL, MAX, MIN = AluOpType.add, AluOpType.subtract, AluOpType.mult, AluOpType.max, AluOpType.min
 COPY, SIGN = ActivationFunctionType.Copy, ActivationFunctionType.Sign
-ABS, RELU = ActivationFunctionType.Abs, ActivationFunctionType.Relu
+ABS, RELU, IDENT = ActivationFunctionType.Abs, ActivationFunctionType.Relu, ActivationFunctionType.Identity
+SHIFT = 2.0 ** 18
 EB0, K512, K3, SG, SGH = 0, 4, 5, 6, 7
 
 
@@ -131,7 +133,7 @@ def rank_program(g, core, T, topo):
             lambda: V.quantize_mx(codes(name, a, b), plane(name, a, b), T[src][:, 4 * a:4 * b]))
 
     def mm(bank, l, la, r, ra, rb, start=True, stop=True):
-        run("t", [(l + "_q", la, la + 128), (r + "_q", ra, rb)], ["ps%d" % bank],
+        run("t", [(l + "_q", la, la + 128), (r + "_q", ra, rb)] + [l + "_s"] * (l[0] == "u"), ["ps%d" % bank],
             lambda: g.tensor.matmul_mx(T["ps%d" % bank][:, 0:rb - ra], codes(l, la, la + 128), plane(l, la, la + 128),
                                        codes(r, ra, rb), plane(r, ra, rb), start, stop))
 
@@ -150,8 +152,8 @@ def rank_program(g, core, T, topo):
     def scan(reads, writes, out, d0, d1, op0, op1):
         run("v", reads, writes, lambda: V.tensor_tensor_scan(out, d0, d1, 0.0, op0, op1))
 
-    def fold(src, dst, n):
-        scan([src, "fold0"], [dst], T[dst][:, 0:n], T.fold0[:, 0:n], T[src][:, 0:n], MUL, ADD)
+    def cut(row, regs, dst, n=C):
+        scan(regs + ["pick"], [dst], T[dst][:, 0:n], T.pick[:, 0:n], row, ADD, MAX)
 
     dma("y", "ldx", [], ["xb"], T.xb[:], T.x[:])
     dma("s", "ldu", [], ["ub"], T.ub[:], T.u[:])
@@ -199,14 +201,19 @@ def rank_program(g, core, T, topo):
     fill("half", 0, 4, 0.5)
     vts([("qg", 0, 2)], [("qg", 4, 6)], T.qg[:, 4:6], T.qg[:, 0:2], -1.0, None, MUL)
     q_of, g_of = T.qg[:, 0:1], T.qg[:, 1:2]
+    shift_of = T.qg[:, 7:8]
     act(["jmod"], ["fold0"], T.fold0[:], T.jmod[:], SIGN)
-    act(["jmod"], ["foldb"], T.foldb[:], T.jmod[:], SIGN)
     act(["jmod", ("qg", 4, 6)], ["mask"], T.mask[:], T.jmod[:], ABS, bias=T.qg[:, 4:5])
     act(["mask"], ["mask"], T.mask[:], T.mask[:], RELU, bias=1.0, scale=-1.0)
 
     def blank(name, first):
         act(["jmod"], [name], T[name][:, first:first + 4 * C - 3:4], T.jmod[:], scale=0.0)
 
+    act([("qg", 0, 2)], [("qg", 8, 9)], T.qg[:, 8:9], q_of, IDENT, bias=-0.5)
+    act(["jmod", ("qg", 8, 9)], ["mbig"], T.mbig[:], T.jmod[:], SIGN, bias=T.qg[:, 8:9], scale=-1.0)
+    act(["mbig"], ["mbig"], T.mbig[:], T.mbig[:], scale=1e29)
+    act([("qg", 0, 2)], [("qg", 6, 7)], T.qg[:, 6:7], q_of, IDENT, bias=1.0)
+    act([("qg", 0, 2)], [("qg", 7, 8)], shift_of, q_of, IDENT, bias=15.0 * SHIFT, scale=-SHIFT)
     blank("le", 3)
     blank("ge", 3)
     for i in (5, 2):
@@ -220,16 +227,18 @@ def rank_program(g, core, T, topo):
             lambda: V.tensor_copy(T[name + "_q"][:, 0:128].bitcast(dt.uint32), T.u_q[:, 0:128].bitcast(dt.uint32).indirect(T[off][:, 0:8])))
 
     repeat("us", "uso")
-    quant("x", "xb")
+    quant("x", "xb", 0, HALF, ["xb"])
+    quant("x", "xb", HALF, C, ["xb"])
     repeat("uh", "uho")
-    vts(["jmod", ("qg", 0, 2)], ["mbig"], T.mbig[:], T.jmod[:], q_of, 2e29, LT, MUL)
     fill("rs", 0, 1, 0.0)
-    vts(["mbig"], ["mbig"], T.mbig[:], T.mbig[:], 1e29, None, SUB)
 
     def packs():
         quant("k", "cb", 512, 768, [("cb", 2048, 3072)])
         quant("k", "cb", 0, 512, [("cb", 0, 2048)])
         vcp(["cfi"], ["cl"], T.cl[:], T.cfi[:])
+        act(["jmod", ("qg", 6, 7)], ["pick"], T.pick[:], T.jmod[:], RELU, bias=T.qg[:, 6:7], scale=-1.0)
+        act(["pick"], ["pick"], T.pick[:], T.pick[:], IDENT, bias=SHIFT, scale=-256.0 * SHIFT)
+        act(["jmod"], ["foldb"], T.foldb[:], T.jmod[:], SIGN)
         act(["g8", ("qg", 4, 6)], ["g8"], T.g8[:], T.g8[:], ABS, bias=T.qg[:, 5:6])
         act(["g8"], [tile(SG)], const(SG), T.g8[:], RELU, bias=1.0, scale=-1.0)
         act(["g8"], [tile(SGH)], const(SGH), T.g8[:], RELU, bias=0.5, scale=-0.5)
@@ -247,9 +256,12 @@ def rank_program(g, core, T, topo):
         vts(["jt"], [("ct0", 0, lead)], T.ct0[:, 0:lead], T.jt[:, 0:lead], -1.0, 383.0 - 8 * (24 - lead), MUL, ADD)
         vts(["jt", ("qg", 0, 2)], [("ct0", lead, 24)], T.ct0[:, lead:24], T.jt[:, lead:24], 0.0, q_of, MUL, SUB)
         vts([("ct0", lead, 24)], [("ct0", lead, 24)], T.ct0[:, lead:24], T.ct0[:, lead:24], 199.0, None, ADD)
+        vts(["ct0", ("qg", 7, 8)], ["ct0"], T.ct0[:], T.ct0[:], shift_of, None, ADD)
+        vts(["jg", ("qg", 7, 8)], ["jg"], T.jg[:], T.jg[:], shift_of, None, SUB)
 
     def products():
-        mm(0, "us", 0, "x", 0, C)
+        mm(0, "us", 0, "x", 0, HALF)
+        mm(7, "us", 0, "x", HALF, C)
         for b in range(3):
             mm(2 + b, "x", 128 * b, "u", 0, 128)
         mm(1, "uh", 0, "x", 0, C)
@@ -260,9 +272,9 @@ def rank_program(g, core, T, topo):
             act(["ps1", ("hs", b, b + 1)], [("sgn", C * b, C * b + C)], pl(T.sgn, b), T.ps1[:, 0:C], SIGN, bias=T.hs[:, b:b + 1], scale=-1.0)
 
     def planes():
-        for t, bank in enumerate((6, 7, 2, 1)):
+        for t, bank in enumerate((6, 2, 1, 7)):
             mm(bank, "k", 128 * (EB0 + t), "x", 0, C)
-        for t, bank in enumerate((6, 7, 2, 1)):
+        for t, bank in enumerate((6, 2, 1, 7)):
             act(["ps%d" % bank], ["fp%d" % t], pl(T.fp, t), T["ps%d" % bank][:, 0:C])
 
     def turning():
@@ -298,9 +310,7 @@ def rank_program(g, core, T, topo):
         mm(6, "k", 128 * K3, "mk", C, 2 * C, False, True)
         yield
         yield
-        vtt(["ps6", "mask"], ["km"], T.km[:], T.ps6[:, 0:C], T.mask[:], MUL)
-        yield
-        scan(["km", "foldb"], ["kf"], T.kf[:], T.foldb[:], T.km[:], MUL, ADD)
+        cut(T.ps6[:, 0:C], ["ps6"], "kf")
         yield
         for i in range(2):
             a, b = 24 * i, 24 * i + 24
@@ -311,10 +321,11 @@ def rank_program(g, core, T, topo):
         vcp(["u1"], ["oab"], T.oab[:], T.u1[:])
         yield
         for i in range(2):
-            a, b, ab, abf = 24 * i, 24 * i + 24, ("ab", C * i, C * i + C), ("abf", C * i, C * i + C)
-            vtt(["win", "oab", "mask"], [ab], pl(T.ab, i), T.win[:, 0:8 * C].indirect(T.oab[:, a:b]), T.mask[:], MUL)
-            yield
-            scan([ab, "fold0"], [abf], pl(T.abf, i), T.fold0[:], pl(T.ab, i), MUL, ADD)
+            act(["win", "oab"], ["ar#%d" % i], pl(T.ar, i), T.win[:, 0:8 * C].indirect(T.oab[:, 24 * i:24 * i + 24]))
+        yield
+        for i in range(2):
+            a, b, abf = 24 * i, 24 * i + 24, ("abf", C * i, C * i + C)
+            scan(["ar#%d" % i, "pick"], [abf], pl(T.abf, i), T.pick[:], pl(T.ar, i), ADD, MAX)
             yield
             vcp([abf], [("ti", a, b)], T.ti[:, a:b], T.abf[:, C * i + 15:C * i + C:16])
             yield
@@ -327,25 +338,24 @@ def rank_program(g, core, T, topo):
             yield
 
     def orders(r):
-        vtt(["ps0", "mask"], ["sm"], T.sm[:], T.ps0[:, 0:C], T.mask[:], MUL)
-        yield
-        vtt(["ps0", "mbig"], ["smk"], T.smk[:], T.ps0[:, 0:C], T.mbig[:], MIN)
-        yield
-        fold("sm", "sf", C)
-        vts(["sf"], ["ns"], T.ns[:], T.sf[:, 15:C:16], -1.0, None, MUL)
+        for dst, by, op in (("sm", "mask", MUL), ("smk", "mbig", MIN)):
+            for a, bank in ((0, "ps0"), (HALF, "ps7")):
+                vtt([bank, by], [(dst, a, a + HALF)], T[dst][:, a:a + HALF], T[bank][:, 0:HALF], T[by][:, a:a + HALF], op)
+            yield
+        scan(["sm", "fold0"], ["sf"], T.sf[:], T.fold0[:], T.sm[:], MUL, ADD)
         act(["sf", "uso"], ["ex"], T.ex[:], T.sf[:, 0:C].indirect(T.uso[:, 8:32]))
         yield
         score = [T.sf[:, 16 * c + 15:16 * c + 16] for c in range(24)]
         for c in range(23, 4 * FIRST - 2, -1):
             if c >= 4 * FIRST:
                 a = C * (c % 12)
-                act(["ps5", "ns"], [("sig", a, a + C)], T.sig[:, a:a + 16 * c], T.ps5[:, 0:16 * c], SIGN, bias=T.ns[:, c:c + 1])
+                act(["ps5", "sf"], [("sig", a, a + C)], T.sig[:, a:a + 16 * c], T.ps5[:, 0:16 * c], SIGN, bias=score[c], scale=-1.0)
             if c < 23:
                 d = c + 1
                 i, t, a = d // 4, d % 4, C * (d % 12)
                 name = "cmp%d" % i
                 act([("sig", a, a + C), "half", name], [name + "#%d" % t, ("rs", d, d + 1)], T[name][:, t:64 * (d - 1) + 60 + t + 1:4],
-                    T.sig[:, a:a + 16 * d], SIGN, bias=T.half[:, 0:1], accum_out=T.rs[:, d:d + 1])
+                    T.sig[:, a:a + 16 * d], SIGN, bias=T.half[:, 0:1], scale=-1.0, accum_out=T.rs[:, d:d + 1])
                 if d == 20:
                     yield
 
@@ -394,9 +404,7 @@ def rank_program(g, core, T, topo):
         yield
         vtt(["rs", "rc"], ["rc"], T.rc[:], T.rs[:], T.rc[:], ADD)
         yield
-        vtt(["ps2", "mask"], ["cm"], T.cm[:], T.ps2[:, 0:C], T.mask[:], MUL)
-        yield
-        fold("cm", "cf2", C)
+        cut(T.ps2[:, 0:C], ["ps2"], "cf2")
         yield
         vtt(["rc", "cf2"], ["rc"], T.rc[:], T.rc[:], T.cf2[:, 15:C:16], SUB)
         yield
@@ -404,11 +412,9 @@ def rank_program(g, core, T, topo):
         yield
         vcp(["iotaj", "pos"], ["inv"], T.inv[:, 0:C].indirect(T.pos[:, 0:24]), T.iotaj[:])
         yield
-        vtt(["inv", "mask"], ["cm"], T.cm[:, 0:M], T.inv[:, 0:M], T.mask[:, 0:M], MUL)
+        cut(T.inv[:, 0:M], ["inv"], "cf2", M)
         yield
-        fold("cm", "cf2", M)
-        yield
-        vcp(["cf2"], ["lo"], T.lo[:], T.cf2[:, 15:M:16])
+        vts(["cf2", ("qg", 7, 8)], ["lo"], T.lo[:], T.cf2[:, 15:M:16], shift_of, None, SUB)
         yield
 
     nxt = T.cores[(rank + 1) % len(T.cores)]
@@ -417,7 +423,7 @@ def rank_program(g, core, T, topo):
 
     for r in range(ROUNDS):
         products()
-        chains = [[orders(r), 34, 0], [turning(), 48, 0]]
+        chains = [[orders(r), 40, 0], [turning(), 48, 0]]
         for _ in range(4):
             next(chains[0][0])
         if r == 0:
@@ -434,7 +440,7 @@ def rank_program(g, core, T, topo):
             vtt(["fc%d" % t, ("at", 24, 48), "ag%d" % t], ["zp%d" % t], pl(T.zp, t), pl(T.fc, t).indirect(T.at[:, 24:48]), pl(T.ag, t), ADD)
         for t in range(4):
             out, in_ = T.eb[:, t:4 * M:4], pl(T.zp, t).indirect(T.lo[:, 0:10])
-            if t < 2:
+            if t < 3:
                 act(["zp%d" % t, "lo"], ["eb#%d" % t], out, in_)
             else:
                 vcp(["zp%d" % t, "lo"], ["eb#%d" % t], out, in_)
@@ -448,12 +454,11 @@ def rank_program(g, core, T, topo):
         for a, b, c in ((0, 224, 384), (160, 160, 224), (224, 0, 160)):
             act(["inv"], [("wrow", a, a + c - b)], T.wrow[:, a:a + c - b], T.inv[:, b:c])
         vcp(["wrow", "pos"], ["swap"], T.swap[:], T.wrow[:, 0:C].indirect(T.pos[:, 0:24]))
+        act(["swap", "cl"], ["crm"], T.crm[:], T.swap[:, 0:C].indirect(T.cl[:, 0:24]))
         if r + 1 < ROUNDS:
-            vtt(["swap", "cl", "mask"], ["crm"], T.crm[:], T.swap[:, 0:C].indirect(T.cl[:, 0:24]), T.mask[:], MUL)
-            fold("crm", "crf", C)
-            vcp(["crf"], ["cl"], T.cl[:], T.crf[:, 15:C:16])
+            cut(T.crm[:], ["crm"], "crf")
+            vts(["crf", ("qg", 7, 8)], ["cl"], T.cl[:], T.crf[:, 15:C:16], shift_of, None, SUB)
         else:
-            vcp(["swap", "cl"], ["crm"], T.crm[:], T.swap[:, 0:C].indirect(T.cl[:, 0:24]))
             dma("y", "stp", ["crm"], [], T.op[:], T.crm[0:128:16, :])
         if r == 0:
             quant("v", "vb")
@@ -470,18 +475,18 @@ def rank_program(g, core, T, topo):
                 act(["ps%d" % banks[b]], [("rz%d" % b, C - M, C)], out, in_, scale=0.03125)
         for b in range(4):
             vtt(["rz%d" % b, "pos", "zp%d" % b], ["xb#%d" % b], T.xb[:, b:4 * C:4], pl(T.rz, b).indirect(T.pos[:, 0:24]), pl(T.zp, b), ADD)
-        quant("x", "xb", 0, C, ["xb#%d" % b for b in range(4)])
+        for a in (0, HALF):
+            quant("x", "xb", a, a + HALF, ["xb#%d" % b for b in range(4)])
 
-    h = C // 2
-    mm(0, "v", 0, "x", 0, h)
-    mm(5, "v", 0, "x", h, C)
+    mm(0, "v", 0, "x", 0, HALF)
+    mm(5, "v", 0, "x", HALF, C)
     dma("y", "stc", ["x_q"], [], T.oc[:], T.x_q[:, 0:C].bitcast(dt.uint8))
     for k in range(4):
         dma("y", "sts%d" % k, ["x_q"], [], T.osc[4 * k:4 * k + 4, :], T.x_s[32 * k:32 * k + 4, 0:C])
-    act(["ps0"], [("yb", 0, h)], T.yb[:, 0:h], T.ps0[:, 0:h])
-    dma("s", "sty", [("yb", 0, h)], [], T.y[:, 0:h], T.yb[:, 0:h])
-    vcp(["ps5"], [("yb", h, C)], T.yb[:, h:C], T.ps5[:, 0:h])
-    dma("s", "sty2", [("yb", h, C)], [], T.y[:, h:C], T.yb[:, h:C])
+    act(["ps0"], [("yb", 0, HALF)], T.yb[:, 0:HALF], T.ps0[:, 0:HALF])
+    dma("s", "sty", [("yb", 0, HALF)], [], T.y[:, 0:HALF], T.yb[:, 0:HALF])
+    vcp(["ps5"], [("yb", HALF, C)], T.yb[:, HALF:C], T.ps5[:, 0:HALF])
+    dma("s", "sty2", [("yb", HALF, C)], [], T.y[:, HALF:C], T.yb[:, HALF:C])
     for s in ("vec", "act", "ten", "pool"):
         g.wait_ge(T.sem[s], count[s])
     for s in ("ldx", "ldu", "ldv", "ldw", "lds", "ldc", "sty", "sty2", "stp", "stc", "sts0", "sts1", "sts2", "sts3"):

from concourse.mybir import dt, AluOpType, ActivationFunctionType

C, M, ROUNDS = 384, 160, 3
HALF = C // 2
FIRST = 3
WIDE = [max(128, 64 * (i + 1)) for i in range(6)]
X4 = "float8_e4m3fn_x4"
F32, BF = "float32", "bfloat16"
SCRATCH = {}


def _buf(name, cols, dtype, where="sbuf"):
    SCRATCH[name] = (where, [128, cols], dtype)


def _pair(name, cols):
    _buf(name + "_q", cols, X4)
    _buf(name + "_s", cols, "uint8")


for _n, _c in (("xb", 4 * C), ("ub", 512), ("vb", 512), ("cb", 8 * 512), ("sig", 12 * C), ("hb", 512), ("dg", 4 * C), ("dr", C),
               ("sgn", 3 * C), ("le", 4 * C), ("ge", 4 * C), ("mk", 8 * C), ("junk", 4 * C), ("eb", 4 * M), ("ones", C),
               ("foldb", C)):
    _buf(_n, _c, BF)
for _n, _c in (("fp", BF), ("fc", BF), ("ag", BF), ("zp", BF), ("rz", F32)):
    _buf(_n, 4 * C, _c)
for _i in range(6):
    _buf("cmp%d" % _i, 4 * WIDE[_i], BF)
for _n, _c in (("iotaj", C), ("crow", C), ("jmod", C), ("g8", 512), ("ex", C), ("jt", 48), ("jg", 48), ("ct0", 24), ("qg", 10),
               ("mask", C), ("fold0", C), ("pick", C), ("mbig", C), ("hs", 4), ("ka", C), ("win", 8 * C), ("u1", 48), ("kf", C),
               ("ar", 2 * C), ("abf", 2 * C), ("sm", C), ("sf", C), ("smk", C), ("rs", 24), ("half", 4), ("rc", 24), ("cf2", C),
               ("inv", C), ("wrow", C), ("swap", C), ("crm", C), ("crf", C), ("yb", C)):
    _buf(_n, _c, F32)
for _n, _c in (("cfi", 24), ("pcol", 4), ("us32", 32), ("ti", 48)):
    _buf(_n, _c, "int32")
for _n, _c in (("uso", 32), ("uho", 8), ("oab", 48), ("at", 48), ("pos", 24), ("lo", 10), ("cl", 24)):
    _buf(_n, _c, "uint16")
for _n, _c in (("u", 128), ("us", 128), ("uh", 128), ("v", 128), ("w", 512), ("x", C), ("k", 8 * 128), ("le", C), ("ge", C),
               ("mk", 2 * C), ("dg", C)):
    _pair(_n, _c)
for _i in range(6):
    _pair("cmp%d" % _i, WIDE[_i])
for _r in range(ROUNDS):
    _pair("e%d" % _r, M)
    _pair("land%d" % _r, M)
for _b in range(8):
    _buf("ps%d" % _b, 512, F32, "psum")
SEMAPHORES = ["vec", "act", "ten", "pool", "sent", "ldx", "ldu", "ldv", "ldw", "lds", "ldc", "sty", "sty2", "stp", "stc",
              "sts0", "sts1", "sts2", "sts3", "arr0", "arr1", "arr2"]

LE, GE, EQ = AluOpType.is_le, AluOpType.is_ge, AluOpType.is_equal
ADD, SUB, MUL, MAX, MIN = AluOpType.add, AluOpType.subtract, AluOpType.mult, AluOpType.max, AluOpType.min
COPY, SIGN = ActivationFunctionType.Copy, ActivationFunctionType.Sign
ABS, RELU, IDENT = ActivationFunctionType.Abs, ActivationFunctionType.Relu, ActivationFunctionType.Identity
SHIFT = 2.0 ** 18
EB0, K512, K3, SG, SGH = 0, 4, 5, 6, 7


def rank_program(g, core, T, topo):
    rank = T.rank_of(core)
    if rank is None:
        return
    queue = {"v": g.vector, "s": g.scalar, "t": g.tensor, "p": g, "y": g.sync}
    own = {"v": "vec", "s": "act", "t": "ten", "p": "pool"}
    count = {"vec": 0, "act": 0, "ten": 0, "pool": 0}
    seen = {q: {} for q in queue}
    clock, hist = {}, {}

    def waits(q, reads, writes):
        need = {}
        for kind, regs in (("r", reads), ("w", writes)):
            for key, lo, hi in regs:
                for a, b, k, q2, ev in hist.get(key, []):
                    if b <= lo or hi <= a:
                        continue
                    if kind == "r" and k == "r" and not (key[:2] == "ps" and q2 != q):
                        continue
                    if kind == "w" and q2 == q and (k == "r" or q == "t"):
                        continue
                    need[ev[0]] = max(need.get(ev[0], 0), ev[1])
        need = {s: n for s, n in need.items() if seen[q].get(s, 0) < n}
        for s in sorted(need):
            if any(o != s and clock[(o, need[o])].get(s, 0) >= need[s] for o in need if need[o]):
                need[s] = 0
        for s, n in need.items():
            if n and seen[q].get(s, 0) < n:
                queue[q].wait_ge(T.sem[s], n)
                for s2, n2 in clock[(s, n)].items():
                    seen[q][s2] = max(seen[q].get(s2, 0), n2)

    def note(q, ev, reads, writes):
        clock[ev] = dict(seen[q] if q in seen else {})
        clock[ev][ev[0]] = ev[1]
        for key, lo, hi in writes:
            hist[key] = [e for e in hist.get(key, []) if not (lo <= e[0] and e[1] <= hi)] + [(lo, hi, "w", q, ev)]
        for key, lo, hi in reads:
            hist[key] = [e for e in hist.get(key, []) if not (e[2] == "r" and e[3] == q and lo <= e[0] and e[1] <= hi)]
            hist[key].append((lo, hi, "r", q, ev))

    def full(regs):
        return [(r, 0, 1 << 20) if not isinstance(r, tuple) else r for r in regs]

    def run(q, reads, writes, call):
        reads, writes = full(reads), full(writes)
        waits(q, reads, writes)
        s = own[q]
        count[s] += 1
        call().then_inc(T.sem[s], 1)
        note(q, (s, count[s]), reads, writes)

    def dma(q, sem, reads, writes, out, in_):
        reads, writes = full(reads), full(writes)
        waits(q, reads, writes)
        queue[q].dma_start(out, in_).then_inc(T.sem[sem], 16)
        saved = dict(seen[q])
        note("d" + sem, (sem, 16), reads, writes)
        clock[(sem, 16)].update(saved)

    V, S, P = g.vector, g.scalar, g

    def pl(buf, t):
        return buf[:, C * t:C * t + C]

    def codes(name, a, b):
        return T[name + "_q"][:, a:b]

    def plane(name, a, b):
        return T[name + "_s"][:, a:b]

    def quant(name, src, a=0, b=None, regs=None):
        b = SCRATCH[name + "_q"][1][1] if b is None else b
        run("v", [src] if regs is None else regs, [name + "_q"] if regs is None else [(name + "_q", a, b)],
            lambda: V.quantize_mx(codes(name, a, b), plane(name, a, b), T[src][:, 4 * a:4 * b]))

    def mm(bank, l, la, r, ra, rb, start=True, stop=True):
        run("t", [(l + "_q", la, la + 128), (r + "_q", ra, rb)] + [l + "_s"] * (l[0] == "u"), ["ps%d" % bank],
            lambda: g.tensor.matmul_mx(T["ps%d" % bank][:, 0:rb - ra], codes(l, la, la + 128), plane(l, la, la + 128),
                                       codes(r, ra, rb), plane(r, ra, rb), start, stop))

    def vts(reads, writes, out, in0, s1, s2, *ops):
        run("v", reads, writes, lambda: V.tensor_scalar(out, in0, s1, s2, *ops))

    def vtt(reads, writes, out, in0, in1, op):
        run("v", reads, writes, lambda: V.tensor_tensor(out, in0, in1, op))

    def vcp(reads, writes, out, in_):
        run("v", reads, writes, lambda: V.tensor_copy(out, in_))

    def act(reads, writes, out, in_, func=COPY, **kw):
        run("s", reads, writes, lambda: S.activation(out, in_, func, **kw))

    def scan(reads, writes, out, d0, d1, op0, op1):
        run("v", reads, writes, lambda: V.tensor_tensor_scan(out, d0, d1, 0.0, op0, op1))

    def cut(row, regs, dst, n=C):
        scan(regs + ["pick"], [dst], T[dst][:, 0:n], T.pick[:, 0:n], row, ADD, MAX)

    dma("y", "ldx", [], ["xb"], T.xb[:], T.x[:])
    dma("s", "ldu", [], ["ub"], T.ub[:], T.u[:])
    dma("s", "ldc", [], ["cfi"], T.cfi[:], T.cf[:])
    dma("s", "ldw", [], ["w_q"], T.w_q[:, 0:512].bitcast(dt.uint8), T.wc[:])
    dma("y", "lds", [], ["w_s"], T.w_s[:], T.ws[:])
    dma("y", "ldv", [], ["vb"], T.vb[:], T.v[:])

    def iota(name, a, b, pattern, base, cm, **kw):
        run("p", [], [(name, a, b)], lambda: P.iota(T[name][:, a:b], pattern, base, cm, **kw))

    def fill(name, a, b, value):
        run("v", [], [(name, a, b)], lambda: V.memset(T[name][:, a:b], value))

    def tile(k):
        return "cb", 512 * k, 512 * k + 512

    def const(k):
        return T.cb[:, 512 * k:512 * k + 512]

    ok = {"allow_small_or_imprecise_dtypes": True}
    iota("us32", 0, 8, [[16, 8]], 0, 0)
    iota("us32", 8, 32, [[16, 24]], 15, 0)
    iota("pcol", 0, 1, [[1, 1]], 0, 1)
    iota("jmod", 0, C, [[0, 24], [1, 16]], 0, 0, **ok)
    iota("jt", 0, 24, [[16, 24]], 0, 0, **ok)
    iota("jt", 24, 48, [[16, 24]], 0, 0, **ok)
    fill("hb", 0, 512, 0.5)
    for t in range(4):
        run("p", ["hb"], [tile(EB0 + t)], lambda: P.affine_select(const(EB0 + t), T.hb[:], [[1, 512]], EQ, 0.0, -t, -4))
    iota("g8", 0, 512, [[1, 8], [0, 64]], 0, 0, **ok)
    iota("crow", 0, C, [[1, C]], -512, 0, **ok)
    for i in (4, 3, 1, 0):
        iota("cmp%d" % i, 256 * i, 4 * WIDE[i], [[0, 4 * WIDE[i] - 256 * i]], 0, 0, **ok)
    iota("iotaj", 0, C, [[1, C]], 0, 0, **ok)

    fill("uho", 0, 8, 1)
    fill(*tile(K512), 512.0)
    fill(*tile(K3), 3.0)
    vcp(["us32"], ["uso"], T.uso[:], T.us32[:])
    vts(["pcol"], [("pcol", 1, 2)], T.pcol[:, 1:2], T.pcol[:, 0:1], 15, None, AluOpType.bitwise_and)
    vts(["pcol"], [("pcol", 2, 3)], T.pcol[:, 2:3], T.pcol[:, 0:1], 4, None, AluOpType.arith_shift_right)
    fill("ones", 0, C, 1.0)
    vcp([("pcol", 1, 3)], [("qg", 0, 2)], T.qg[:, 0:2], T.pcol[:, 1:3])
    fill("half", 0, 4, 0.5)
    vts([("qg", 0, 2)], [("qg", 4, 6)], T.qg[:, 4:6], T.qg[:, 0:2], -1.0, None, MUL)
    q_of, g_of = T.qg[:, 0:1], T.qg[:, 1:2]
    shift_of = T.qg[:, 7:8]
    act(["jmod"], ["fold0"], T.fold0[:], T.jmod[:], SIGN)
    act(["jmod", ("qg", 4, 6)], ["mask"], T.mask[:], T.jmod[:], ABS, bias=T.qg[:, 4:5])
    act(["mask"], ["mask"], T.mask[:], T.mask[:], RELU, bias=1.0, scale=-1.0)

    def blank(name, first):
        act(["jmod"], [name], T[name][:, first:first + 4 * C - 3:4], T.jmod[:], scale=0.0)

    act([("qg", 0, 2)], [("qg", 8, 9)], T.qg[:, 8:9], q_of, IDENT, bias=-0.5)
    act(["jmod", ("qg", 8, 9)], ["mbig"], T.mbig[:], T.jmod[:], SIGN, bias=T.qg[:, 8:9], scale=-1.0)
    act(["mbig"], ["mbig"], T.mbig[:], T.mbig[:], scale=1e29)
    act([("qg", 0, 2)], [("qg", 6, 7)], T.qg[:, 6:7], q_of, IDENT, bias=1.0)
    act([("qg", 0, 2)], [("qg", 7, 8)], shift_of, q_of, IDENT, bias=15.0 * SHIFT, scale=-SHIFT)
    blank("le", 3)
    blank("ge", 3)
    for i in (5, 2):
        fill("cmp%d" % i, 256 * i, 4 * WIDE[i], 0.0)
    fill("dg", 0, 4 * C, 0.0)
    quant("u", "ub")

    def repeat(name, off):
        run("v", ["u_q", off], [name + "_s"], lambda: V.tensor_copy(T[name + "_s"][:, 0:128], T.u_s[:, 0:128].indirect(T[off][:, 0:8])))
        run("v", ["u_q", off], [name + "_q"],
            lambda: V.tensor_copy(T[name + "_q"][:, 0:128].bitcast(dt.uint32), T.u_q[:, 0:128].bitcast(dt.uint32).indirect(T[off][:, 0:8])))

    repeat("us", "uso")
    quant("x", "xb", 0, HALF, ["xb"])
    quant("x", "xb", HALF, C, ["xb"])
    repeat("uh", "uho")
    fill("rs", 0, 1, 0.0)

    def packs():
        quant("k", "cb", 512, 768, [("cb", 2048, 3072)])
        quant("k", "cb", 0, 512, [("cb", 0, 2048)])
        vcp(["cfi"], ["cl"], T.cl[:], T.cfi[:])
        act(["jmod", ("qg", 6, 7)], ["pick"], T.pick[:], T.jmod[:], RELU, bias=T.qg[:, 6:7], scale=-1.0)
        act(["pick"], ["pick"], T.pick[:], T.pick[:], IDENT, bias=SHIFT, scale=-256.0 * SHIFT)
        act(["jmod"], ["foldb"], T.foldb[:], T.jmod[:], SIGN)
        act(["g8", ("qg", 4, 6)], ["g8"], T.g8[:], T.g8[:], ABS, bias=T.qg[:, 5:6])
        act(["g8"], [tile(SG)], const(SG), T.g8[:], RELU, bias=1.0, scale=-1.0)
        act(["g8"], [tile(SGH)], const(SGH), T.g8[:], RELU, bias=0.5, scale=-0.5)

    def tables():
        lead = 4 * FIRST
        blank("mk", 4 * C + 3)
        for t in range(4):
            act(["jmod"], [("rz%d" % t, 0, C - M)], T.rz[:, C * t:C * t + C - M], T.jmod[:, 0:C - M], scale=0.0)
        vts(["jt", ("qg", 0, 2)], ["jt"], T.jt[:], T.jt[:], q_of, None, ADD)
        vts([("qg", 0, 2)], [("qg", 2, 3)], T.qg[:, 2:3], g_of, 384.0, None, MUL)
        vts([("qg", 0, 2)], [("qg", 3, 4)], T.qg[:, 3:4], g_of, 384.0, 384.0, MUL, ADD)
        vts(["jt", ("qg", 2, 3)], [("jg", 0, 24)], T.jg[:, 0:24], T.jt[:, 0:24], T.qg[:, 2:3], None, SUB)
        vts(["jt", ("qg", 3, 4)], [("jg", 24, 48)], T.jg[:, 24:48], T.jt[:, 24:48], T.qg[:, 3:4], None, SUB)
        vts(["jt"], [("ct0", 0, lead)], T.ct0[:, 0:lead], T.jt[:, 0:lead], -1.0, 383.0 - 8 * (24 - lead), MUL, ADD)
        vts(["jt", ("qg", 0, 2)], [("ct0", lead, 24)], T.ct0[:, lead:24], T.jt[:, lead:24], 0.0, q_of, MUL, SUB)
        vts([("ct0", lead, 24)], [("ct0", lead, 24)], T.ct0[:, lead:24], T.ct0[:, lead:24], 199.0, None, ADD)
        vts(["ct0", ("qg", 7, 8)], ["ct0"], T.ct0[:], T.ct0[:], shift_of, None, ADD)
        vts(["jg", ("qg", 7, 8)], ["jg"], T.jg[:], T.jg[:], shift_of, None, SUB)

    def products():
        mm(0, "us", 0, "x", 0, HALF)
        mm(7, "us", 0, "x", HALF, C)
        for b in range(3):
            mm(2 + b, "x", 128 * b, "u", 0, 128)
        mm(1, "uh", 0, "x", 0, C)
        mm(5, "us", 0, "x", 0, C)
        for b in range(3):
            act(["ps%d" % (2 + b)], [("hs", b, b + 1)], T.hs[:, b:b + 1], T["ps%d" % (2 + b)][:, 1:2])
        for b in range(3):
            act(["ps1", ("hs", b, b + 1)], [("sgn", C * b, C * b + C)], pl(T.sgn, b), T.ps1[:, 0:C], SIGN, bias=T.hs[:, b:b + 1], scale=-1.0)

    def planes():
        for t, bank in enumerate((6, 2, 1, 7)):
            mm(bank, "k", 128 * (EB0 + t), "x", 0, C)
        for t, bank in enumerate((6, 2, 1, 7)):
            act(["ps%d" % bank], ["fp%d" % t], pl(T.fp, t), T["ps%d" % bank][:, 0:C])

    def turning():
        for name, op, bank in (("le", LE, 3), ("ge", GE, 4)):
            for b in range(3):
                vts([("sgn", C * b, C * b + C)], [name + "#%d" % b], T[name][:, b:4 * C:4], pl(T.sgn, b), 0.0, None, op)
                yield
            quant(name, name, 0, C, [name + "#%d" % b for b in range(3)] + [name])
            mm(bank, "k", 128 * K512, name, 0, C)
            yield
        vtt(["ps3", "crow"], ["ka"], T.ka[:], T.ps3[:, 0:C], T.crow[:], ADD)
        yield
        for m in range(7):
            even = m % 2 == 0
            key = T.ka[:] if even else T.win[:, 7 * C:8 * C]
            last = T.ones[:] if m == 0 else T.mk[:, mark:mark + 4 * (C - 1) + 1:4]
            scan(["ka" if even else ("win", 7 * C, 8 * C), "ones" if m == 0 else "mk#%d" % (m - 1)], [("win", C * m, C * m + C)],
                 pl(T.win, m), last, key, MUL, MAX)
            yield
            if m == 0:
                vtt(["ps4", "crow"], [("win", 7 * C, 8 * C)], pl(T.win, 7), T.ps4[:, 0:C], T.crow[:], ADD)
                yield
            mark = m if m < 4 else 4 * C + m - 4
            bank = 3 if even else 4
            vtt(["ps%d" % bank, ("win", C * m, C * m + C)], ["mk#%d" % m], T.mk[:, mark:mark + 4 * (C - 1) + 1:4],
                pl(T.win, m), T["ps%d" % bank][:, 0:C], GE)
            yield
            if m == 3:
                quant("mk", "mk", 0, C, ["mk#%d" % i for i in range(4)])
                mm(6, "k", 128 * K3, "mk", 0, C, True, False)
                yield
        quant("mk", "mk", C, 2 * C, ["mk#%d" % i for i in range(4, 7)] + ["mk"])
        mm(6, "k", 128 * K3, "mk", C, 2 * C, False, True)
        yield
        yield
        cut(T.ps6[:, 0:C], ["ps6"], "kf")
        yield
        for i in range(2):
            a, b = 24 * i, 24 * i + 24
            vtt(["kf", ("jg", a, b)], [("u1", a, b)], T.u1[:, a:b], T.kf[:, 15:C:16], T.jg[:, a:b], ADD)
            yield
        vtt(["u1", "jt"], ["u1"], T.u1[:], T.u1[:], T.jt[:], MAX)
        yield
        vcp(["u1"], ["oab"], T.oab[:], T.u1[:])
        yield
        for i in range(2):
            act(["win", "oab"], ["ar#%d" % i], pl(T.ar, i), T.win[:, 0:8 * C].indirect(T.oab[:, 24 * i:24 * i + 24]))
        yield
        for i in range(2):
            a, b, abf = 24 * i, 24 * i + 24, ("abf", C * i, C * i + C)
            scan(["ar#%d" % i, "pick"], [abf], pl(T.abf, i), T.pick[:], pl(T.ar, i), ADD, MAX)
            yield
            vcp([abf], [("ti", a, b)], T.ti[:, a:b], T.abf[:, C * i + 15:C * i + C:16])
            yield
            vts([("ti", a, b)], [("ti", a, b)], T.ti[:, a:b], T.ti[:, a:b], 511, None, AluOpType.bitwise_and)
            yield
            vcp([("ti", a, b)], [("at", a, b)], T.at[:, a:b], T.ti[:, a:b])
            if i == 0:
                for t in range(4):
                    act(["fc%d" % t, ("at", a, b)], ["ag%d" % t], pl(T.ag, t), pl(T.fc, t).indirect(T.at[:, a:b]))
            yield

    def orders(r):
        for dst, by, op in (("sm", "mask", MUL), ("smk", "mbig", MIN)):
            for a, bank in ((0, "ps0"), (HALF, "ps7")):
                vtt([bank, by], [(dst, a, a + HALF)], T[dst][:, a:a + HALF], T[bank][:, 0:HALF], T[by][:, a:a + HALF], op)
            yield
        scan(["sm", "fold0"], ["sf"], T.sf[:], T.fold0[:], T.sm[:], MUL, ADD)
        act(["sf", "uso"], ["ex"], T.ex[:], T.sf[:, 0:C].indirect(T.uso[:, 8:32]))
        yield
        score = [T.sf[:, 16 * c + 15:16 * c + 16] for c in range(24)]
        for c in range(23, 4 * FIRST - 2, -1):
            if c >= 4 * FIRST:
                a = C * (c % 12)
                act(["ps5", "sf"], [("sig", a, a + C)], T.sig[:, a:a + 16 * c], T.ps5[:, 0:16 * c], SIGN, bias=score[c], scale=-1.0)
            if c < 23:
                d = c + 1
                i, t, a = d // 4, d % 4, C * (d % 12)
                name = "cmp%d" % i
                act([("sig", a, a + C), "half", name], [name + "#%d" % t, ("rs", d, d + 1)], T[name][:, t:64 * (d - 1) + 60 + t + 1:4],
                    T.sig[:, a:a + 16 * d], SIGN, bias=T.half[:, 0:1], scale=-1.0, accum_out=T.rs[:, d:d + 1])
                if d == 20:
                    yield

        def counts(name, half, cols, first=False, last=False):
            mm(2, "k", 128 * (SGH if half else SG), name, 0, cols, first, last)

        def pack(i):
            name = "cmp%d" % i
            quant(name, name, 0, WIDE[i], [name + "#%d" % t for t in range(4)] + [name])
            counts(name, i >= FIRST, WIDE[i], i == 5, i == FIRST)

        for i in range(FIRST - 1, -1, -1):
            name = "cmp%d" % i
            for t in range(3, -1, -1):
                c = 4 * i + t
                if c:
                    part, end = name + "#%d" % t, 64 * (c - 1) + 60 + t + 1
                    vts(["ps0", "sf", name], [part], T[name][:, t:end:4], T.ps0[:, 0:16 * c], score[c], None, GE)
                    act([part], [("junk", C * t, C * t + C), ("rs", c, c + 1)], T.junk[:, C * t:C * t + 16 * c], T[name][:, t:end:4],
                        accum_out=T.rs[:, c:c + 1])
                    yield
            if i == FIRST - 1:
                vtt(["smk", "ex", "dg"], ["dg#0"], T.dg[:, 0:4 * C - 3:4], T.smk[:], T.ex[:], GE)
                yield
        if r == 0:
            quant("k", "cb", 768, 1024, [("cb", 3072, 4096)])
            yield
        pack(5)
        yield
        quant("dg", "dg", 0, C, ["dg#0", "dg"])
        counts("dg", False, C)
        yield
        scan(["dg#0", "foldb"], ["dr"], T.dr[:], T.foldb[:], T.dg[:, 0:4 * C - 3:4], MUL, ADD)
        yield
        vtt(["ct0", "dr"], ["rc"], T.rc[:], T.ct0[:], T.dr[:, 15:C:16], ADD)
        yield
        for i in range(FIRST - 1, -1, -1):
            pack(i)
            yield
        for t in range(4):
            act(["fp%d" % t, "cl"], ["fc%d" % t], pl(T.fc, t), pl(T.fp, t).indirect(T.cl[:, 0:24]))
        for i in range(4, FIRST - 1, -1):
            pack(i)
            yield
        vts([("rs", 4 * FIRST, 24)], [("rs", 4 * FIRST, 24)], T.rs[:, 4 * FIRST:24], T.rs[:, 4 * FIRST:24], 0.5, None, MUL)
        yield
        vtt(["rs", "rc"], ["rc"], T.rc[:], T.rs[:], T.rc[:], ADD)
        yield
        cut(T.ps2[:, 0:C], ["ps2"], "cf2")
        yield
        vtt(["rc", "cf2"], ["rc"], T.rc[:], T.rc[:], T.cf2[:, 15:C:16], SUB)
        yield
        vcp(["rc"], ["pos"], T.pos[:], T.rc[:])
        yield
        vcp(["iotaj", "pos"], ["inv"], T.inv[:, 0:C].indirect(T.pos[:, 0:24]), T.iotaj[:])
        yield
        cut(T.inv[:, 0:M], ["inv"], "cf2", M)
        yield
        vts(["cf2", ("qg", 7, 8)], ["lo"], T.lo[:], T.cf2[:, 15:M:16], shift_of, None, SUB)
        yield

    nxt = T.cores[(rank + 1) % len(T.cores)]
    rid, pid = topo.addr(nxt)[:2]
    engines = len(topo.engines(core, nxt))

    for r in range(ROUNDS):
        products()
        chains = [[orders(r), 40, 0], [turning(), 48, 0]]
        for _ in range(4):
            next(chains[0][0])
        if r == 0:
            packs()
        planes()
        if r == 0:
            tables()
        while chains:
            c = min(chains, key=lambda e: e[2] / e[1])
            c[2] += 1
            if next(c[0], 0) == 0:
                chains.remove(c)
        for t in range(4):
            vtt(["fc%d" % t, ("at", 24, 48), "ag%d" % t], ["zp%d" % t], pl(T.zp, t), pl(T.fc, t).indirect(T.at[:, 24:48]), pl(T.ag, t), ADD)
        for t in range(4):
            out, in_ = T.eb[:, t:4 * M:4], pl(T.zp, t).indirect(T.lo[:, 0:10])
            if t < 3:
                act(["zp%d" % t, "lo"], ["eb#%d" % t], out, in_)
            else:
                vcp(["zp%d" % t, "lo"], ["eb#%d" % t], out, in_)
        name, land, arr = "e%d" % r, "land%d" % r, "arr%d" % r
        quant(name, "eb", 0, M, ["eb#%d" % t for t in range(4)])
        waits("p", full([name + "_q"]), [])
        g.remote_dma(T[land + "_q"][:, 0:M].bitcast(dt.uint8), T[name + "_q"][:, 0:M].bitcast(dt.uint8), T.sem[arr], T.sem.sent, pid, rid,
                     topo.mask(core, nxt))
        g.remote_dma(T[land + "_s"][:, 0:M], T[name + "_s"][:, 0:M], T.sem[arr], T.sem.sent, pid, rid, topo.mask(core, nxt))
        note("d" + arr, (arr, 2 * engines), [], full([land + "_q"]))
        for a, b, c in ((0, 224, 384), (160, 160, 224), (224, 0, 160)):
            act(["inv"], [("wrow", a, a + c - b)], T.wrow[:, a:a + c - b], T.inv[:, b:c])
        vcp(["wrow", "pos"], ["swap"], T.swap[:], T.wrow[:, 0:C].indirect(T.pos[:, 0:24]))
        act(["swap", "cl"], ["crm"], T.crm[:], T.swap[:, 0:C].indirect(T.cl[:, 0:24]))
        if r + 1 < ROUNDS:
            cut(T.crm[:], ["crm"], "crf")
            vts(["crf", ("qg", 7, 8)], ["cl"], T.cl[:], T.crf[:, 15:C:16], shift_of, None, SUB)
        else:
            dma("y", "stp", ["crm"], [], T.op[:], T.crm[0:128:16, :])
        if r == 0:
            quant("v", "vb")
        banks = (1, 2, 6, 7)
        for b in range(4):
            run("t", ["w_q", "w_s", land + "_q"], ["ps%d" % banks[b]],
                lambda: g.tensor.matmul_mx(T["ps%d" % banks[b]][:, 0:M], codes("w", 128 * b, 128 * b + 128), plane("w", 128 * b, 128 * b + 128),
                                           codes(land, 0, M), plane(land, 0, M), True, True))
        for b in range(4):
            out, in_ = T.rz[:, C * b + C - M:C * b + C], T["ps%d" % banks[b]][:, 0:M]
            if b == 0:
                vts(["ps%d" % banks[b]], [("rz%d" % b, C - M, C)], out, in_, 0.03125, None, MUL)
            else:
                act(["ps%d" % banks[b]], [("rz%d" % b, C - M, C)], out, in_, scale=0.03125)
        for b in range(4):
            vtt(["rz%d" % b, "pos", "zp%d" % b], ["xb#%d" % b], T.xb[:, b:4 * C:4], pl(T.rz, b).indirect(T.pos[:, 0:24]), pl(T.zp, b), ADD)
        for a in (0, HALF):
            quant("x", "xb", a, a + HALF, ["xb#%d" % b for b in range(4)])

    mm(0, "v", 0, "x", 0, HALF)
    mm(5, "v", 0, "x", HALF, C)
    dma("y", "stc", ["x_q"], [], T.oc[:], T.x_q[:, 0:C].bitcast(dt.uint8))
    for k in range(4):
        dma("y", "sts%d" % k, ["x_q"], [], T.osc[4 * k:4 * k + 4, :], T.x_s[32 * k:32 * k + 4, 0:C])
    act(["ps0"], [("yb", 0, HALF)], T.yb[:, 0:HALF], T.ps0[:, 0:HALF])
    dma("s", "sty", [("yb", 0, HALF)], [], T.y[:, 0:HALF], T.yb[:, 0:HALF])
    vcp(["ps5"], [("yb", HALF, C)], T.yb[:, HALF:C], T.ps5[:, 0:HALF])
    dma("s", "sty2", [("yb", HALF, C)], [], T.y[:, HALF:C], T.yb[:, HALF:C])
    for s in ("vec", "act", "ten", "pool"):
        g.wait_ge(T.sem[s], count[s])
    for s in ("ldx", "ldu", "ldv", "ldw", "lds", "ldc", "sty", "sty2", "stp", "stc", "sts0", "sts1", "sts2", "sts3"):
        g.wait_ge(T.sem[s], 16)
    g.wait_ge(T.sem.sent, 2 * engines * ROUNDS)
